import numpy as np
import ml_dtypes


def mxq(x, axis, fmt="e4m3"):
    dtype, down = {"e4m3": (ml_dtypes.float8_e4m3fn, 7), "e5m2": (ml_dtypes.float8_e5m2, 14)}[fmt]
    v = np.moveaxis(np.asarray(x, np.float32).astype(ml_dtypes.bfloat16).astype(np.float64), axis, -1)
    blocks = v.reshape(v.shape[:-1] + (-1, 32))
    amax = np.abs(blocks).max(-1, keepdims=True)
    byte = np.maximum(np.where(amax > 0, np.frexp(amax)[1] - 1 + 127, 0) - down, 1)
    scale = np.exp2(byte - 127.0)
    codes = (blocks / scale).astype(np.float32).astype(dtype).astype(np.float64)
    return np.moveaxis((codes * scale).reshape(v.shape), -1, axis)


WIDE = False


def mx_kscale(k):
    if not WIDE:
        return np.ones(k)
    levels = np.array([10, -10, 5, -5, 0])
    if k % 512:
        return np.exp2(np.random.permutation(np.resize(levels, k // 32))).repeat(32)
    a = np.empty((k // 512, 16))
    for p in range(k // 512):
        a[p, :8] = np.random.permutation(np.resize(levels, 8))
        for g in range(8):
            far = levels[np.abs(levels - a[p, g]) >= 10]
            a[p, g + 8] = far[np.random.randint(len(far))]
    return np.exp2(a.ravel()).repeat(32)


def f64(x):
    return np.asarray(x).astype(np.float64)


def striped(idx):
    return np.tile(idx.reshape(-1, 16).T, (8, 1)).astype(np.uint16)


def unstriped(offs):
    return offs[:16].T.reshape(-1).astype(np.int64)


def striped8(idx):
    return np.concatenate([x.reshape(-1, 16).T for x in idx]).astype(np.uint16)


def runs(offs, k):
    lists = np.stack([offs[16 * r : 16 * r + 16].T.reshape(-1) for r in range(8)]).astype(np.int64)
    return lists[np.arange(k) % 512 // 64]


def pack_weight(w):
    k, n = w.shape
    w = f64(np.asarray(w, np.float32).astype(ml_dtypes.bfloat16)).reshape(k // 32, 32, n)
    amax = np.abs(w).max(1)
    byte = np.clip(np.where(amax > 0, np.frexp(amax)[1] - 1 + 127 - 7, 1), 1, 254)
    scaled = (w * np.exp2(127.0 - byte)[:, None, :]).reshape(k, n).astype(np.float32)
    words = np.ascontiguousarray(scaled.reshape(k // 512, 128, 4, n).transpose(0, 1, 3, 2)).astype(ml_dtypes.float8_e4m3fn).view(np.uint8)
    return words, np.ascontiguousarray(byte.astype(np.uint8).reshape(k // 512, 16, n))


def unpack_weight(words, scales):
    g, p, n, _ = words.shape
    vals = np.ascontiguousarray(words).view(ml_dtypes.float8_e4m3fn).astype(np.float64) * np.repeat(np.exp2(scales.astype(np.float64) - 127.0), 8, axis=1)[..., None]
    return vals.transpose(0, 1, 3, 2).reshape(g * 512, n)


E2M1 = np.array([0.0, 0.5, 1.0, 1.5, 2.0, 3.0, 4.0, 6.0, -0.0, -0.5, -1.0, -1.5, -2.0, -3.0, -4.0, -6.0])


def pack_fp4(w):
    k, n = w.shape
    w = f64(np.asarray(w, np.float32).astype(ml_dtypes.bfloat16)).reshape(k // 32, 32, n)
    amax = np.abs(w).max(1)
    mant, ex = np.frexp(amax / 6.0)
    byte = np.clip(np.where(amax > 0, np.where(mant > 0.5, ex, ex - 1) + 127, 1), 1, 254)
    scaled = (w * np.exp2(127.0 - byte)[:, None, :]).reshape(k, n).astype(np.float32)
    c = np.ascontiguousarray(scaled.reshape(k // 512, 128, 4, n).transpose(0, 1, 3, 2)).astype(ml_dtypes.float4_e2m1fn).view(np.uint8) & 0xF
    words = (c[..., 0::2] | (c[..., 1::2] << 4)).reshape(k // 512, 128, 2 * n)
    return np.ascontiguousarray(words), np.ascontiguousarray(byte.astype(np.uint8).reshape(k // 512, 16, n))


def unpack_fp4(words, scales):
    g, _, n = scales.shape
    words = np.ascontiguousarray(words).reshape(g, 128, n, 2)
    nib = np.empty((g, 128, n, 4), np.uint8)
    nib[..., 0::2] = words & 0xF
    nib[..., 1::2] = words >> 4
    vals = E2M1[nib] * np.repeat(np.exp2(scales.astype(np.float64) - 127.0), 8, axis=1)[..., None]
    return vals.transpose(0, 1, 3, 2).reshape(g * 512, n)


def relu(v):
    return np.maximum(v, 0.0)

def planes(y):
    n, m = y.shape
    v = y.astype(np.float32).astype(ml_dtypes.bfloat16).astype(np.float64).reshape(n // 32, 32, m)
    top = np.abs(v).max(1)
    byte = np.clip(np.where(top > 0, np.frexp(top)[1] - 1 + 127 - 7, 1), 1, 254)
    codes = (v * np.exp2(127.0 - byte)[:, None, :]).reshape(n, m).astype(np.float32).astype(ml_dtypes.float8_e4m3fn).view(np.uint8)
    words = codes.reshape(n // 512, 128, 4, m).transpose(0, 1, 3, 2)
    return np.ascontiguousarray(words), np.ascontiguousarray(byte.astype(np.uint8).reshape(n // 512, 16, m))


K, T, S, N, U, H = 512, 2048, 512, 512, 1024, 512


def setup_inputs():
    n = np.random.standard_normal
    s = mx_kscale(K)[:, None]
    u = mx_kscale(H)
    packed_xT = pack_weight(n((K, T)) * s)
    packed_w2 = pack_fp4(n((H, N)) / np.sqrt(H) / u[:, None])
    return {
        "x_words": packed_xT[0],
        "x_scales": packed_xT[1],
        "w1": (n((K, H)) / np.sqrt(K) / s * u).astype(np.float32),
        "b1": (0.5 * n((H, 1)) * u[:, None]).astype(np.float32),
        "w2_words": packed_w2[0],
        "w2_scales": packed_w2[1],
        "b2": (0.5 * n((N, 1))).astype(np.float32),
        "offs": striped(np.random.permutation(T)[:S]),
        "held": striped8(np.stack([np.random.permutation(U)[:S] for _ in range(8)])),
    }


def reference(x_words, x_scales, w1, b1, w2_words, w2_scales, b2, offs, held):
    xq = unpack_weight(x_words, x_scales)[:, unstriped(offs)]
    y = relu((mxq(f64(w1), 0, "e4m3").T @ xq) + f64(b1))
    z = np.zeros((H, U))
    z[np.arange(H)[:, None], runs(held, H)] = y
    out_0 = (unpack_fp4(w2_words, w2_scales).T @ mxq(z, 0, "e4m3")) + f64(b2)
    return (out_0,) + planes(out_0)

@@ -1,0 +1,193 @@
+from contextlib import ExitStack
+
+import concourse.mybir as mybir
+
+K, T, S, H, U, N = 512, 2048, 512, 512, 1024, 512
+FLOPS = 2 * K * H * S + 2 * H * N * U
+
+F32 = mybir.dt.float32
+BF16 = mybir.dt.bfloat16
+I32 = mybir.dt.int32
+U32 = mybir.dt.uint32
+U16 = mybir.dt.uint16
+U8 = mybir.dt.uint8
+FP8X4 = mybir.dt.float8_e4m3fn_x4
+FP4X4 = mybir.dt.float4_e2m1fn_x4
+ACT = mybir.ActivationFunctionType
+
+P = 128
+PACK = 4
+BANK = 512
+HALF = S // 2
+CHUNKS = (128, 256, 256, 256, 128)
+
+
+def tile_picked_sae8_relu_po_kernel(
+    tc, x_words, x_scales, w1, b1, w2_words, w2_scales, b2, offs, held, out_0, out_1, out_2
+):
+    nc = tc.nc
+    starts = [sum(CHUNKS[:c]) for c in range(len(CHUNKS))]
+    last = len(CHUNKS) - 1
+
+    with ExitStack() as ctx:
+        lists = ctx.enter_context(tc.tile_pool(name="lists", bufs=1))
+        sb = ctx.enter_context(tc.tile_pool(name="sb", bufs=1))
+        psum = ctx.enter_context(tc.psum_pool(name="psum", bufs=1))
+
+        offs_sb = lists.tile([P, S // 16], U16, name="offs_sb")
+        held_sb = lists.tile([P, S // 16], U16, name="held_sb")
+        w1_raw = sb.tile([P, PACK, H], F32, name="w1_raw", align_bytes=64)
+        x_tab = sb.tile([P, T], U32, name="x_tab", align_bytes=64)
+        xs_tab = sb.tile([P, T], U8, name="xs_tab", align_bytes=64)
+        w2_raw = sb.tile([P, 2 * N], U8, name="w2_raw", align_bytes=64)
+        w2s_raw = sb.tile([P, N], U8, name="w2s_raw", align_bytes=64)
+        b1_sb = sb.tile([P, PACK], F32, name="b1_sb")
+        b2_sb = sb.tile([P, PACK], F32, name="b2_sb")
+        z = [sb.tile([P, U], F32, name=f"z{t}", align_bytes=64) for t in range(PACK)]
+
+        nc.vector.memset(xs_tab[:].bitcast(I32), 0)
+        nc.vector.memset(w2s_raw[:].bitcast(I32), 0)
+
+        nc.sync.dma_start(offs_sb[:], offs)
+        nc.scalar.dma_start(w2_raw[:].bitcast(I32), w2_words[0].bitcast(I32))
+        nc.sync.dma_start(held_sb[:], held)
+        nc.sync.dma_start(w1_raw[:], w1.rearrange("(p j) c -> p j c", j=PACK))
+        nc.sync.dma_start(x_tab[:].bitcast(I32), x_words[0].rearrange("p c r -> p (c r)").bitcast(I32))
+        for q in range(4):
+            nc.scalar.dma_start(xs_tab[32 * q : 32 * q + 4, :].bitcast(I32), x_scales[0, 4 * q : 4 * q + 4, :].bitcast(I32))
+        for q in range(4):
+            queue = nc.scalar if q < 2 else nc.gpsimd
+            queue.dma_start(w2s_raw[32 * q : 32 * q + 4, :].bitcast(I32), w2_scales[0, 4 * q : 4 * q + 4, :].bitcast(I32))
+        nc.gpsimd.dma_start(b1_sb[:], b1.rearrange("(p t) o -> p (t o)", t=PACK))
+        nc.gpsimd.dma_start(b2_sb[:], b2.rearrange("(p t) o -> p (t o)", t=PACK))
+
+        for t in range(PACK):
+            nc.vector.memset(z[t][:], 0.0)
+
+        xs_pick = sb.tile([P, S], U8, name="xs_pick", align_bytes=64)
+        nc.vector.tensor_copy(xs_pick[:], xs_tab[:].indirect(offs_sb[:]))
+
+        w2_deal = sb.tile([P, 2 * N], U8, name="w2_deal", align_bytes=64)
+        nc.vector.tensor_copy(
+            w2_deal[:].rearrange("p (t m b) -> p m t b", t=PACK, b=2),
+            w2_raw[:].rearrange("p (m t b) -> p m t b", t=PACK, b=2),
+        )
+
+        w1_src = w1_raw[:].rearrange("p j (m t) -> p m j t", t=PACK)
+        w1_codes, w1_scales = [], []
+        for h in range(2):
+            grouped = sb.tile([P, 2, P, PACK], BF16, name=f"w1_bf{h}", align_bytes=64)
+            dst = grouped[:].rearrange("p t m j -> p m j t")
+            src = w1_src[:, :, :, 2 * h : 2 * h + 2]
+            if h == 0:
+                nc.vector.tensor_copy(dst, src)
+            else:
+                nc.scalar.copy(dst, src)
+            codes = sb.tile([P, 2 * P], U32, name=f"w1_codes{h}", align_bytes=64)
+            scales = sb.tile([P, 2 * P], U8, name=f"w1_scales{h}", align_bytes=64)
+            nc.vector.quantize_mx(codes[:].bitcast(FP8X4), scales[:], grouped[:].rearrange("p t m j -> p (t m j)"))
+            w1_codes.append(codes)
+            w1_scales.append(scales)
+
+        w2s_deal = sb.tile([P, N], U8, name="w2s_deal", align_bytes=64)
+        nc.vector.tensor_copy(
+            w2s_deal[:].rearrange("p (t m) -> p m t", t=PACK),
+            w2s_raw[:].rearrange("p (m t) -> p m t", t=PACK),
+        )
+
+        x_pick = sb.tile([P, S], U32, name="x_pick", align_bytes=64)
+        for h in range(2):
+            nc.vector.tensor_copy(
+                x_pick[:, h * HALF : (h + 1) * HALF],
+                x_tab[:].indirect(offs_sb[:, h * HALF // 16 : (h + 1) * HALF // 16]),
+            )
+
+        y = [sb.tile([P, S], F32, name=f"y{t}", align_bytes=64) for t in range(PACK)]
+        pieces = [(0, 0, HALF), (0, HALF, S)] + [(t, 0, S) for t in range(1, PACK)]
+        for i, (t, lo, hi) in enumerate(pieces):
+            acc = psum.tile([P, BANK], F32, name=f"acc1_{i}", tag=f"bank{i}")
+            cols = slice((t % 2) * P, (t % 2 + 1) * P)
+            nc.tensor.matmul_mx(
+                out=acc[:, 0 : hi - lo],
+                lhsT=w1_codes[t // 2][:, cols].bitcast(FP8X4),
+                lhsT_scale=w1_scales[t // 2][:, cols],
+                rhs=x_pick[:, lo:hi].bitcast(FP8X4),
+                rhs_scale=xs_pick[:, lo:hi],
+                start=True,
+                stop=True,
+            )
+            nc.scalar.activation(y[t][:, lo:hi], acc[:, 0 : hi - lo], ACT.Relu, bias=b1_sb[:, t : t + 1])
+
+        z_bf = [sb.tile([P, n, PACK], BF16, name=f"z_bf{c}", align_bytes=64) for c, n in enumerate(CHUNKS)]
+        for t, lo, hi in pieces:
+            nc.vector.tensor_copy(z[t][:].indirect(held_sb[:, lo // 16 : hi // 16]), y[t][:, lo:hi])
+            if hi == S and t < PACK - 1:
+                for c, n in enumerate(CHUNKS):
+                    plane = z[t][:, starts[c] : starts[c] + n]
+                    if t == PACK - 2 and c < last:
+                        nc.scalar.copy(z_bf[c][:, :, t:PACK], plane.unsqueeze(2).to_broadcast([P, n, 2]))
+                    else:
+                        nc.scalar.copy(z_bf[c][:, :, t], plane)
+
+        nc.scalar.copy(z_bf[last][:, :, PACK - 1], z[PACK - 1][:, starts[last] : U])
+
+        out_words = sb.tile([P, U], U32, name="out_words", align_bytes=64)
+        out_scales = sb.tile([P, U], U8, name="out_scales", align_bytes=64)
+        out_rows = out_0.rearrange("(p t) w -> p t w", t=PACK)
+        out_1_rows = out_1[0].rearrange("p c r -> p (c r)").bitcast(I32)
+
+        z_codes = [sb.tile([P, n], U32, name=f"z_codes{c}", align_bytes=64) for c, n in enumerate(CHUNKS)]
+        z_scales = [sb.tile([P, n], U8, name=f"z_scales{c}", align_bytes=64) for c, n in enumerate(CHUNKS)]
+        res = [sb.tile([P, PACK, n], F32, name=f"res{c}", align_bytes=64) for c, n in enumerate(CHUNKS)]
+        res_bf = [sb.tile([P, n, PACK], BF16, name=f"res_bf{c}", align_bytes=64) for c, n in enumerate(CHUNKS)]
+
+        def last_plane(c):
+            nc.vector.tensor_copy(z_bf[c][:, :, PACK - 1], z[PACK - 1][:, starts[c] : starts[c] + CHUNKS[c]])
+
+        def decode(c):
+            n = CHUNKS[c]
+            nc.vector.quantize_mx(z_codes[c][:].bitcast(FP8X4), z_scales[c][:], z_bf[c][:].rearrange("p n t -> p (n t)"))
+            per_bank = BANK // n
+            for b in range(PACK // per_bank):
+                bank = PACK * starts[c] // BANK + b
+                acc = psum.tile([P, BANK], F32, name=f"acc2_{bank}", tag=f"bank{bank}")
+                for i in range(per_bank):
+                    t = b * per_bank + i
+                    nc.tensor.matmul_mx(
+                        out=acc[:, i * n : (i + 1) * n],
+                        lhsT=w2_deal[:, 2 * P * t : 2 * P * (t + 1)].bitcast(FP4X4),
+                        lhsT_scale=w2s_deal[:, P * t : P * (t + 1)],
+                        rhs=z_codes[c][:].bitcast(FP8X4),
+                        rhs_scale=z_scales[c][:],
+                        start=True,
+                        stop=True,
+                    )
+                for i in range(per_bank):
+                    t = b * per_bank + i
+                    nc.scalar.activation(res[c][:, t, :], acc[:, i * n : (i + 1) * n], ACT.Identity, bias=b2_sb[:, t : t + 1])
+            nc.sync.dma_start(out_rows[:, :, starts[c] : starts[c] + n], res[c][:])
+
+        def round_result(c):
+            nc.vector.tensor_copy(
+                res_bf[c][:].rearrange("p (g i) t -> p g t i", i=4),
+                res[c][:].rearrange("p t (g i) -> p g t i", i=4),
+            )
+
+        def hand_on(c):
+            cols = slice(starts[c], starts[c] + CHUNKS[c])
+            nc.vector.quantize_mx(out_words[:, cols].bitcast(FP8X4), out_scales[:, cols], res_bf[c][:].rearrange("p n t -> p (n t)"))
+            nc.sync.dma_start(out_1_rows[:, cols], out_words[:, cols].bitcast(I32))
+
+        last_plane(0)
+        for c in range(len(CHUNKS)):
+            if c + 1 < last:
+                last_plane(c + 1)
+            decode(c)
+        round_result(0)
+        for c in range(len(CHUNKS)):
+            if c < last:
+                round_result(c + 1)
+            hand_on(c)
+        for q in range(4):
+            queue = nc.sync if q % 2 == 0 else nc.scalar
+            queue.dma_start(out_2[0, 4 * q : 4 * q + 4, :].bitcast(I32), out_scales[32 * q : 32 * q + 4, :].bitcast(I32))

@@ -20,6 +20,7 @@ PACK = 4
 BANK = 512
 HALF = S // 2
 CHUNKS = (128, 256, 256, 256, 128)
+SPLIT = 896
 
 
 def tile_picked_sae8_relu_po_kernel(
@@ -45,32 +46,35 @@ def tile_picked_sae8_relu_po_kernel(
         b2_sb = sb.tile([P, PACK], F32, name="b2_sb")
         z = [sb.tile([P, U], F32, name=f"z{t}", align_bytes=64) for t in range(PACK)]
 
-        nc.vector.memset(xs_tab[:].bitcast(I32), 0)
+        xs_rows = sb.tile([P, T], U8, name="xs_rows", align_bytes=64)
+        nc.gpsimd.memset(xs_tab[:].bitcast(I32), 0)
         nc.vector.memset(w2s_raw[:].bitcast(I32), 0)
 
+        for q in range(4):
+            nc.sync.dma_start(xs_rows[32 * q : 32 * q + 4, :].bitcast(I32), x_scales[0, 4 * q : 4 * q + 4, :].bitcast(I32))
         nc.sync.dma_start(offs_sb[:], offs)
-        nc.scalar.dma_start(w2_raw[:].bitcast(I32), w2_words[0].bitcast(I32))
-        nc.sync.dma_start(held_sb[:], held)
+        nc.sync.dma_start(w2_raw[:].bitcast(I32), w2_words[0].bitcast(I32))
         nc.sync.dma_start(w1_raw[:], w1.rearrange("(p j) c -> p j c", j=PACK))
         nc.sync.dma_start(x_tab[:].bitcast(I32), x_words[0].rearrange("p c r -> p (c r)").bitcast(I32))
+        nc.sync.dma_start(b1_sb[:], b1.rearrange("(p t) o -> p (t o)", t=PACK))
+        nc.sync.dma_start(held_sb[:], held)
         for q in range(4):
-            nc.scalar.dma_start(xs_tab[32 * q : 32 * q + 4, :].bitcast(I32), x_scales[0, 4 * q : 4 * q + 4, :].bitcast(I32))
-        for q in range(4):
-            queue = nc.scalar if q < 2 else nc.gpsimd
-            queue.dma_start(w2s_raw[32 * q : 32 * q + 4, :].bitcast(I32), w2_scales[0, 4 * q : 4 * q + 4, :].bitcast(I32))
-        nc.gpsimd.dma_start(b1_sb[:], b1.rearrange("(p t) o -> p (t o)", t=PACK))
-        nc.gpsimd.dma_start(b2_sb[:], b2.rearrange("(p t) o -> p (t o)", t=PACK))
+            nc.sync.dma_start(w2s_raw[32 * q : 32 * q + 4, :].bitcast(I32), w2_scales[0, 4 * q : 4 * q + 4, :].bitcast(I32))
+        nc.sync.dma_start(b2_sb[:], b2.rearrange("(p t) o -> p (t o)", t=PACK))
 
         for t in range(PACK):
-            nc.vector.memset(z[t][:], 0.0)
+            clearer = nc.vector if t < 2 else nc.gpsimd
+            clearer.memset(z[t][:], 0.0)
 
+        for q in range(4):
+            nc.vector.tensor_copy(xs_tab[32 * q : 32 * q + 4, :].bitcast(I32), xs_rows[32 * q : 32 * q + 4, :].bitcast(I32))
         xs_pick = sb.tile([P, S], U8, name="xs_pick", align_bytes=64)
         nc.vector.tensor_copy(xs_pick[:], xs_tab[:].indirect(offs_sb[:]))
 
         w2_deal = sb.tile([P, 2 * N], U8, name="w2_deal", align_bytes=64)
         nc.vector.tensor_copy(
-            w2_deal[:].rearrange("p (t m b) -> p m t b", t=PACK, b=2),
-            w2_raw[:].rearrange("p (m t b) -> p m t b", t=PACK, b=2),
+            w2_deal[:].rearrange("p (t m b) -> p t m b", t=PACK, b=2),
+            w2_raw[:].rearrange("p (m t b) -> p t m b", t=PACK, b=2),
         )
 
         w1_src = w1_raw[:].rearrange("p j (m t) -> p m j t", t=PACK)
@@ -80,20 +84,15 @@ def tile_picked_sae8_relu_po_kernel(
             dst = grouped[:].rearrange("p t m j -> p m j t")
             src = w1_src[:, :, :, 2 * h : 2 * h + 2]
             if h == 0:
-                nc.vector.tensor_copy(dst, src)
-            else:
                 nc.scalar.copy(dst, src)
+            else:
+                nc.scalar.copy(dst[:, 0 : P // 2], src[:, 0 : P // 2])
+                nc.vector.tensor_copy(dst[:, P // 2 : P], src[:, P // 2 : P])
             codes = sb.tile([P, 2 * P], U32, name=f"w1_codes{h}", align_bytes=64)
             scales = sb.tile([P, 2 * P], U8, name=f"w1_scales{h}", align_bytes=64)
             nc.vector.quantize_mx(codes[:].bitcast(FP8X4), scales[:], grouped[:].rearrange("p t m j -> p (t m j)"))
             w1_codes.append(codes)
             w1_scales.append(scales)
-
-        w2s_deal = sb.tile([P, N], U8, name="w2s_deal", align_bytes=64)
-        nc.vector.tensor_copy(
-            w2s_deal[:].rearrange("p (t m) -> p m t", t=PACK),
-            w2s_raw[:].rearrange("p (m t) -> p m t", t=PACK),
-        )
 
         x_pick = sb.tile([P, S], U32, name="x_pick", align_bytes=64)
         for h in range(2):
@@ -101,6 +100,12 @@ def tile_picked_sae8_relu_po_kernel(
                 x_pick[:, h * HALF : (h + 1) * HALF],
                 x_tab[:].indirect(offs_sb[:, h * HALF // 16 : (h + 1) * HALF // 16]),
             )
+
+        w2s_deal = sb.tile([P, N], U8, name="w2s_deal", align_bytes=64)
+        nc.vector.tensor_copy(
+            w2s_deal[:].rearrange("p (t m) -> p t m", t=PACK),
+            w2s_raw[:].rearrange("p (m t) -> p t m", t=PACK),
+        )
 
         y = [sb.tile([P, S], F32, name=f"y{t}", align_bytes=64) for t in range(PACK)]
         pieces = [(0, 0, HALF), (0, HALF, S)] + [(t, 0, S) for t in range(1, PACK)]
@@ -118,18 +123,19 @@ def tile_picked_sae8_relu_po_kernel(
             )
             nc.scalar.activation(y[t][:, lo:hi], acc[:, 0 : hi - lo], ACT.Relu, bias=b1_sb[:, t : t + 1])
 
-        z_bf = [sb.tile([P, n, PACK], BF16, name=f"z_bf{c}", align_bytes=64) for c, n in enumerate(CHUNKS)]
+        z_bf = sb.tile([P, U * PACK], BF16, name="z_bf", align_bytes=64)
+        z_slots = z_bf[:].rearrange("p (w t) -> p w t", t=PACK)
         for t, lo, hi in pieces:
             nc.vector.tensor_copy(z[t][:].indirect(held_sb[:, lo // 16 : hi // 16]), y[t][:, lo:hi])
-            if hi == S and t < PACK - 1:
-                for c, n in enumerate(CHUNKS):
-                    plane = z[t][:, starts[c] : starts[c] + n]
-                    if t == PACK - 2 and c < last:
-                        nc.scalar.copy(z_bf[c][:, :, t:PACK], plane.unsqueeze(2).to_broadcast([P, n, 2]))
-                    else:
-                        nc.scalar.copy(z_bf[c][:, :, t], plane)
+            if hi == S and t < PACK - 2:
+                nc.scalar.copy(z_slots[:, :, t], z[t][:])
+            if t == PACK - 2:
+                for w0 in range(0, SPLIT, SPLIT // 2):
+                    w1_ = w0 + SPLIT // 2
+                    nc.scalar.copy(z_slots[:, w0:w1_, t:PACK], z[t][:, w0:w1_].unsqueeze(2).to_broadcast([P, SPLIT // 2, 2]))
+                nc.scalar.copy(z_slots[:, SPLIT:U, t], z[t][:, SPLIT:U])
 
-        nc.scalar.copy(z_bf[last][:, :, PACK - 1], z[PACK - 1][:, starts[last] : U])
+        nc.scalar.copy(z_slots[:, SPLIT:U, PACK - 1], z[PACK - 1][:, SPLIT:U])
 
         out_words = sb.tile([P, U], U32, name="out_words", align_bytes=64)
         out_scales = sb.tile([P, U], U8, name="out_scales", align_bytes=64)
@@ -142,29 +148,25 @@ def tile_picked_sae8_relu_po_kernel(
         res_bf = [sb.tile([P, n, PACK], BF16, name=f"res_bf{c}", align_bytes=64) for c, n in enumerate(CHUNKS)]
 
         def last_plane(c):
-            nc.vector.tensor_copy(z_bf[c][:, :, PACK - 1], z[PACK - 1][:, starts[c] : starts[c] + CHUNKS[c]])
+            cols = slice(starts[c], min(starts[c] + CHUNKS[c], SPLIT))
+            nc.vector.tensor_copy(z_slots[:, cols, PACK - 1], z[PACK - 1][:, cols])
 
         def decode(c):
             n = CHUNKS[c]
-            nc.vector.quantize_mx(z_codes[c][:].bitcast(FP8X4), z_scales[c][:], z_bf[c][:].rearrange("p n t -> p (n t)"))
-            per_bank = BANK // n
-            for b in range(PACK // per_bank):
-                bank = PACK * starts[c] // BANK + b
-                acc = psum.tile([P, BANK], F32, name=f"acc2_{bank}", tag=f"bank{bank}")
-                for i in range(per_bank):
-                    t = b * per_bank + i
-                    nc.tensor.matmul_mx(
-                        out=acc[:, i * n : (i + 1) * n],
-                        lhsT=w2_deal[:, 2 * P * t : 2 * P * (t + 1)].bitcast(FP4X4),
-                        lhsT_scale=w2s_deal[:, P * t : P * (t + 1)],
-                        rhs=z_codes[c][:].bitcast(FP8X4),
-                        rhs_scale=z_scales[c][:],
-                        start=True,
-                        stop=True,
-                    )
-                for i in range(per_bank):
-                    t = b * per_bank + i
-                    nc.scalar.activation(res[c][:, t, :], acc[:, i * n : (i + 1) * n], ACT.Identity, bias=b2_sb[:, t : t + 1])
+            nc.vector.quantize_mx(z_codes[c][:].bitcast(FP8X4), z_scales[c][:], z_bf[:, PACK * starts[c] : PACK * (starts[c] + n)])
+            for t in range(PACK):
+                bank = (PACK * c + t) % 8
+                acc = psum.tile([P, BANK], F32, name=f"acc2_{c}_{t}", tag=f"bank{bank}")
+                nc.tensor.matmul_mx(
+                    out=acc[:, 0:n],
+                    lhsT=w2_deal[:, 2 * P * t : 2 * P * (t + 1)].bitcast(FP4X4),
+                    lhsT_scale=w2s_deal[:, P * t : P * (t + 1)],
+                    rhs=z_codes[c][:].bitcast(FP8X4),
+                    rhs_scale=z_scales[c][:],
+                    start=True,
+                    stop=True,
+                )
+                nc.scalar.activation(res[c][:, t, :], acc[:, 0:n], ACT.Identity, bias=b2_sb[:, t : t + 1])
             nc.sync.dma_start(out_rows[:, :, starts[c] : starts[c] + n], res[c][:])
 
         def round_result(c):
@@ -178,10 +180,9 @@ def tile_picked_sae8_relu_po_kernel(
             nc.vector.quantize_mx(out_words[:, cols].bitcast(FP8X4), out_scales[:, cols], res_bf[c][:].rearrange("p n t -> p (n t)"))
             nc.sync.dma_start(out_1_rows[:, cols], out_words[:, cols].bitcast(I32))
 
-        last_plane(0)
         for c in range(len(CHUNKS)):
-            if c + 1 < last:
-                last_plane(c + 1)
+            if c < last:
+                last_plane(c)
             decode(c)
         round_result(0)
         for c in range(len(CHUNKS)):

@@ -51,13 +51,13 @@ def tile_picked_sae8_relu_po_kernel(
         nc.vector.memset(w2s_raw[:].bitcast(I32), 0)
 
         for q in range(4):
-            nc.sync.dma_start(xs_rows[32 * q : 32 * q + 4, :].bitcast(I32), x_scales[0, 4 * q : 4 * q + 4, :].bitcast(I32))
+            nc.scalar.dma_start(xs_rows[32 * q : 32 * q + 4, :].bitcast(I32), x_scales[0, 4 * q : 4 * q + 4, :].bitcast(I32))
         nc.sync.dma_start(offs_sb[:], offs)
         nc.sync.dma_start(w2_raw[:].bitcast(I32), w2_words[0].bitcast(I32))
+        nc.sync.dma_start(held_sb[:], held)
         nc.sync.dma_start(w1_raw[:], w1.rearrange("(p j) c -> p j c", j=PACK))
         nc.sync.dma_start(x_tab[:].bitcast(I32), x_words[0].rearrange("p c r -> p (c r)").bitcast(I32))
         nc.sync.dma_start(b1_sb[:], b1.rearrange("(p t) o -> p (t o)", t=PACK))
-        nc.sync.dma_start(held_sb[:], held)
         for q in range(4):
             nc.sync.dma_start(w2s_raw[32 * q : 32 * q + 4, :].bitcast(I32), w2_scales[0, 4 * q : 4 * q + 4, :].bitcast(I32))
         nc.sync.dma_start(b2_sb[:], b2.rearrange("(p t) o -> p (t o)", t=PACK))
@@ -178,7 +178,9 @@ def tile_picked_sae8_relu_po_kernel(
         def hand_on(c):
             cols = slice(starts[c], starts[c] + CHUNKS[c])
             nc.vector.quantize_mx(out_words[:, cols].bitcast(FP8X4), out_scales[:, cols], res_bf[c][:].rearrange("p n t -> p (n t)"))
-            nc.sync.dma_start(out_1_rows[:, cols], out_words[:, cols].bitcast(I32))
+            if c >= 2:
+                stored = slice(0 if c == 2 else starts[c], starts[c] + CHUNKS[c])
+                nc.sync.dma_start(out_1_rows[:, stored], out_words[:, stored].bitcast(I32))
 
         for c in range(len(CHUNKS)):
             if c < last:

@@ -47,24 +47,23 @@ def tile_picked_sae8_relu_po_kernel(
         z = [sb.tile([P, U], F32, name=f"z{t}", align_bytes=64) for t in range(PACK)]
 
         xs_rows = sb.tile([P, T], U8, name="xs_rows", align_bytes=64)
-        nc.gpsimd.memset(xs_tab[:].bitcast(I32), 0)
+        nc.vector.memset(xs_tab[:].bitcast(I32), 0)
         nc.vector.memset(w2s_raw[:].bitcast(I32), 0)
 
-        for q in range(4):
-            nc.scalar.dma_start(xs_rows[32 * q : 32 * q + 4, :].bitcast(I32), x_scales[0, 4 * q : 4 * q + 4, :].bitcast(I32))
         nc.sync.dma_start(offs_sb[:], offs)
-        nc.sync.dma_start(w2_raw[:].bitcast(I32), w2_words[0].bitcast(I32))
-        nc.sync.dma_start(held_sb[:], held)
+        for q in range(4):
+            nc.sync.dma_start(xs_rows[32 * q : 32 * q + 4, :].bitcast(I32), x_scales[0, 4 * q : 4 * q + 4, :].bitcast(I32))
+        nc.scalar.dma_start(w2_raw[:].bitcast(I32), w2_words[0].bitcast(I32))
         nc.sync.dma_start(w1_raw[:], w1.rearrange("(p j) c -> p j c", j=PACK))
         nc.sync.dma_start(x_tab[:].bitcast(I32), x_words[0].rearrange("p c r -> p (c r)").bitcast(I32))
         nc.sync.dma_start(b1_sb[:], b1.rearrange("(p t) o -> p (t o)", t=PACK))
+        nc.sync.dma_start(held_sb[:], held)
         for q in range(4):
             nc.sync.dma_start(w2s_raw[32 * q : 32 * q + 4, :].bitcast(I32), w2_scales[0, 4 * q : 4 * q + 4, :].bitcast(I32))
         nc.sync.dma_start(b2_sb[:], b2.rearrange("(p t) o -> p (t o)", t=PACK))
 
         for t in range(PACK):
-            clearer = nc.vector if t < 2 else nc.gpsimd
-            clearer.memset(z[t][:], 0.0)
+            nc.vector.memset(z[t][:], 0.0)
 
         for q in range(4):
             nc.vector.tensor_copy(xs_tab[32 * q : 32 * q + 4, :].bitcast(I32), xs_rows[32 * q : 32 * q + 4, :].bitcast(I32))

@@ -37,32 +37,25 @@ def tile_picked_sae8_relu_po_kernel(
 
         offs_sb = lists.tile([P, S // 16], U16, name="offs_sb")
         held_sb = lists.tile([P, S // 16], U16, name="held_sb")
-        w1_raw = sb.tile([P, PACK, H], F32, name="w1_raw", align_bytes=64)
+        w1_raw = sb.tile([P, PACK, H], F32, name="w1_raw", tag="raw", align_bytes=64)
         x_tab = sb.tile([P, T], U32, name="x_tab", align_bytes=64)
         xs_tab = sb.tile([P, T], U8, name="xs_tab", align_bytes=64)
-        w2_raw = sb.tile([P, 2 * N], U8, name="w2_raw", align_bytes=64)
-        w2s_raw = sb.tile([P, N], U8, name="w2s_raw", align_bytes=64)
         b1_sb = sb.tile([P, PACK], F32, name="b1_sb")
-        b2_sb = sb.tile([P, PACK], F32, name="b2_sb")
-        z = [sb.tile([P, U], F32, name=f"z{t}", align_bytes=64) for t in range(PACK)]
-
+        z = [sb.tile([P, U], F32, name=f"z{t}", align_bytes=64) for t in range(2)]
         xs_rows = sb.tile([P, T], U8, name="xs_rows", align_bytes=64)
+
         nc.vector.memset(xs_tab[:].bitcast(I32), 0)
-        nc.vector.memset(w2s_raw[:].bitcast(I32), 0)
 
         nc.sync.dma_start(offs_sb[:], offs)
         for q in range(4):
-            nc.sync.dma_start(xs_rows[32 * q : 32 * q + 4, :].bitcast(I32), x_scales[0, 4 * q : 4 * q + 4, :].bitcast(I32))
-        nc.scalar.dma_start(w2_raw[:].bitcast(I32), w2_words[0].bitcast(I32))
+            queue = nc.sync if q == 0 else nc.scalar
+            queue.dma_start(xs_rows[32 * q : 32 * q + 4, :].bitcast(I32), x_scales[0, 4 * q : 4 * q + 4, :].bitcast(I32))
         nc.sync.dma_start(w1_raw[:], w1.rearrange("(p j) c -> p j c", j=PACK))
-        nc.sync.dma_start(x_tab[:].bitcast(I32), x_words[0].rearrange("p c r -> p (c r)").bitcast(I32))
-        nc.sync.dma_start(b1_sb[:], b1.rearrange("(p t) o -> p (t o)", t=PACK))
         nc.sync.dma_start(held_sb[:], held)
-        for q in range(4):
-            nc.sync.dma_start(w2s_raw[32 * q : 32 * q + 4, :].bitcast(I32), w2_scales[0, 4 * q : 4 * q + 4, :].bitcast(I32))
-        nc.sync.dma_start(b2_sb[:], b2.rearrange("(p t) o -> p (t o)", t=PACK))
+        nc.sync.dma_start(b1_sb[:], b1.rearrange("(p t) o -> p (t o)", t=PACK))
+        nc.sync.dma_start(x_tab[:].bitcast(I32), x_words[0].rearrange("p c r -> p (c r)").bitcast(I32))
 
-        for t in range(PACK):
+        for t in range(2):
             nc.vector.memset(z[t][:], 0.0)
 
         for q in range(4):
@@ -70,23 +63,13 @@ def tile_picked_sae8_relu_po_kernel(
         xs_pick = sb.tile([P, S], U8, name="xs_pick", align_bytes=64)
         nc.vector.tensor_copy(xs_pick[:], xs_tab[:].indirect(offs_sb[:]))
 
-        w2_deal = sb.tile([P, 2 * N], U8, name="w2_deal", align_bytes=64)
-        nc.vector.tensor_copy(
-            w2_deal[:].rearrange("p (t m b) -> p t m b", t=PACK, b=2),
-            w2_raw[:].rearrange("p (m t b) -> p t m b", t=PACK, b=2),
-        )
-
         w1_src = w1_raw[:].rearrange("p j (m t) -> p m j t", t=PACK)
         w1_codes, w1_scales = [], []
         for h in range(2):
-            grouped = sb.tile([P, 2, P, PACK], BF16, name=f"w1_bf{h}", align_bytes=64)
+            grouped = sb.tile([P, 2, P, PACK], BF16, name=f"w1_bf{h}", tag=f"stage{h}", align_bytes=64)
             dst = grouped[:].rearrange("p t m j -> p m j t")
             src = w1_src[:, :, :, 2 * h : 2 * h + 2]
-            if h == 0:
-                nc.scalar.copy(dst, src)
-            else:
-                nc.scalar.copy(dst[:, 0 : P // 2], src[:, 0 : P // 2])
-                nc.vector.tensor_copy(dst[:, P // 2 : P], src[:, P // 2 : P])
+            nc.scalar.copy(dst, src)
             codes = sb.tile([P, 2 * P], U32, name=f"w1_codes{h}", align_bytes=64)
             scales = sb.tile([P, 2 * P], U8, name=f"w1_scales{h}", align_bytes=64)
             nc.vector.quantize_mx(codes[:].bitcast(FP8X4), scales[:], grouped[:].rearrange("p t m j -> p (t m j)"))
@@ -100,13 +83,28 @@ def tile_picked_sae8_relu_po_kernel(
                 x_tab[:].indirect(offs_sb[:, h * HALF // 16 : (h + 1) * HALF // 16]),
             )
 
+        w2_raw = sb.tile([P, 2 * N], U8, name="w2_raw", tag="raw", align_bytes=64)
+        w2s_raw = sb.tile([P, N], U8, name="w2s_raw", tag="stage0", align_bytes=64)
+        w2_deal = sb.tile([P, 2 * N], U8, name="w2_deal", align_bytes=64)
+        z.append(sb.tile([P, U], F32, name="z2", tag="stage1", align_bytes=64))
+        nc.gpsimd.memset(z[2][:], 0.0)
         w2s_deal = sb.tile([P, N], U8, name="w2s_deal", align_bytes=64)
-        nc.vector.tensor_copy(
+        nc.sync.dma_start(w2_raw[:].bitcast(I32), w2_words[0].bitcast(I32))
+        nc.gpsimd.memset(w2s_raw[:].bitcast(I32), 0)
+        for q in range(4):
+            nc.sync.dma_start(w2s_raw[32 * q : 32 * q + 4, :].bitcast(I32), w2_scales[0, 4 * q : 4 * q + 4, :].bitcast(I32))
+        nc.gpsimd.tensor_copy(
+            w2_deal[:].rearrange("p (t m b) -> p t m b", t=PACK, b=2),
+            w2_raw[:].rearrange("p (m t b) -> p t m b", t=PACK, b=2),
+        )
+        nc.gpsimd.tensor_copy(
             w2s_deal[:].rearrange("p (t m) -> p t m", t=PACK),
             w2s_raw[:].rearrange("p (m t) -> p t m", t=PACK),
         )
+        b2_sb = sb.tile([P, PACK], F32, name="b2_sb", tag="stage0", align_bytes=64)
+        nc.sync.dma_start(b2_sb[:], b2.rearrange("(p t) o -> p (t o)", t=PACK))
 
-        y = [sb.tile([P, S], F32, name=f"y{t}", align_bytes=64) for t in range(PACK)]
+        y = [sb.tile([P, S], F32, name=f"y{t}", tag=f"y{t}", align_bytes=64) for t in range(PACK)]
         pieces = [(0, 0, HALF), (0, HALF, S)] + [(t, 0, S) for t in range(1, PACK)]
         for i, (t, lo, hi) in enumerate(pieces):
             acc = psum.tile([P, BANK], F32, name=f"acc1_{i}", tag=f"bank{i}")
@@ -126,6 +124,9 @@ def tile_picked_sae8_relu_po_kernel(
         z_slots = z_bf[:].rearrange("p (w t) -> p w t", t=PACK)
         for t, lo, hi in pieces:
             nc.vector.tensor_copy(z[t][:].indirect(held_sb[:, lo // 16 : hi // 16]), y[t][:, lo:hi])
+            if hi == S and t == 0:
+                z.append(sb.tile([P, U], F32, name="z3", tag="y0", align_bytes=64))
+                nc.gpsimd.memset(z[3][:], 0.0)
             if hi == S and t < PACK - 2:
                 nc.scalar.copy(z_slots[:, :, t], z[t][:])
             if t == PACK - 2:

@@ -14,13 +14,14 @@ U8 = mybir.dt.uint8
 FP8X4 = mybir.dt.float8_e4m3fn_x4
 FP4X4 = mybir.dt.float4_e2m1fn_x4
 ACT = mybir.ActivationFunctionType
+ALU = mybir.AluOpType
 
 P = 128
 PACK = 4
 BANK = 512
 HALF = S // 2
 CHUNKS = (128, 256, 256, 256, 128)
-SPLIT = 896
+SPLIT = 768
 
 
 def tile_picked_sae8_relu_po_kernel(
@@ -128,12 +129,15 @@ def tile_picked_sae8_relu_po_kernel(
                 z.append(sb.tile([P, U], F32, name="z3", tag="y0", align_bytes=64))
                 nc.gpsimd.memset(z[3][:], 0.0)
             if hi == S and t < PACK - 2:
-                nc.scalar.copy(z_slots[:, :, t], z[t][:])
+                nc.scalar.copy(z_slots[:, 0:SPLIT, t], z[t][:, 0:SPLIT])
+                nc.gpsimd.tensor_scalar(z_slots[:, SPLIT:U, t], z[t][:, SPLIT:U], 1.0, 0.0, op0=ALU.mult, op1=ALU.add)
             if t == PACK - 2:
                 for w0 in range(0, SPLIT, SPLIT // 2):
                     w1_ = w0 + SPLIT // 2
                     nc.scalar.copy(z_slots[:, w0:w1_, t:PACK], z[t][:, w0:w1_].unsqueeze(2).to_broadcast([P, SPLIT // 2, 2]))
-                nc.scalar.copy(z_slots[:, SPLIT:U, t], z[t][:, SPLIT:U])
+                nc.gpsimd.tensor_scalar(
+                    z_slots[:, SPLIT:U, t:PACK], z[t][:, SPLIT:U].unsqueeze(2).to_broadcast([P, U - SPLIT, 2]), 1.0, 0.0, op0=ALU.mult, op1=ALU.add
+                )
 
         nc.scalar.copy(z_slots[:, SPLIT:U, PACK - 1], z[PACK - 1][:, SPLIT:U])
 
@@ -167,7 +171,9 @@ def tile_picked_sae8_relu_po_kernel(
                     stop=True,
                 )
                 nc.scalar.activation(res[c][:, t, :], acc[:, 0:n], ACT.Identity, bias=b2_sb[:, t : t + 1])
-            nc.sync.dma_start(out_rows[:, :, starts[c] : starts[c] + n], res[c][:])
+                planes = 2 if c < 2 else PACK
+                if (t + 1) % planes == 0:
+                    nc.sync.dma_start(out_rows[:, t + 1 - planes : t + 1, starts[c] : starts[c] + n], res[c][:, t + 1 - planes : t + 1, :])
 
         def round_result(c):
             nc.vector.tensor_copy(
@@ -178,12 +184,12 @@ def tile_picked_sae8_relu_po_kernel(
         def hand_on(c):
             cols = slice(starts[c], starts[c] + CHUNKS[c])
             nc.vector.quantize_mx(out_words[:, cols].bitcast(FP8X4), out_scales[:, cols], res_bf[c][:].rearrange("p n t -> p (n t)"))
-            if c >= 2:
-                stored = slice(0 if c == 2 else starts[c], starts[c] + CHUNKS[c])
+            if c in (1, 3, last):
+                stored = slice({1: 0, 3: starts[2], last: starts[last]}[c], starts[c] + CHUNKS[c])
                 nc.sync.dma_start(out_1_rows[:, stored], out_words[:, stored].bitcast(I32))
 
         for c in range(len(CHUNKS)):
-            if c < last:
+            if starts[c] < SPLIT:
                 last_plane(c)
             decode(c)
         round_result(0)

@@ -20,6 +20,7 @@ P = 128
 PACK = 4
 BANK = 512
 HALF = S // 2
+FIRST = 128
 CHUNKS = (128, 256, 256, 256, 128)
 SPLIT = 768
 
@@ -106,19 +107,21 @@ def tile_picked_sae8_relu_po_kernel(
         nc.sync.dma_start(b2_sb[:], b2.rearrange("(p t) o -> p (t o)", t=PACK))
 
         y = [sb.tile([P, S], F32, name=f"y{t}", tag=f"y{t}", align_bytes=64) for t in range(PACK)]
-        pieces = [(0, 0, HALF), (0, HALF, S)] + [(t, 0, S) for t in range(1, PACK)]
+        pieces = [(0, 0, FIRST), (1, 0, HALF), (0, FIRST, S), (1, HALF, S), (2, 0, S), (3, 0, S)]
         for i, (t, lo, hi) in enumerate(pieces):
             acc = psum.tile([P, BANK], F32, name=f"acc1_{i}", tag=f"bank{i}")
             cols = slice((t % 2) * P, (t % 2 + 1) * P)
-            nc.tensor.matmul_mx(
-                out=acc[:, 0 : hi - lo],
-                lhsT=w1_codes[t // 2][:, cols].bitcast(FP8X4),
-                lhsT_scale=w1_scales[t // 2][:, cols],
-                rhs=x_pick[:, lo:hi].bitcast(FP8X4),
-                rhs_scale=xs_pick[:, lo:hi],
-                start=True,
-                stop=True,
-            )
+            cuts = [lo, HALF, hi] if lo == FIRST else [lo, hi]
+            for n0, n1 in zip(cuts, cuts[1:]):
+                nc.tensor.matmul_mx(
+                    out=acc[:, n0 - lo : n1 - lo],
+                    lhsT=w1_codes[t // 2][:, cols].bitcast(FP8X4),
+                    lhsT_scale=w1_scales[t // 2][:, cols],
+                    rhs=x_pick[:, n0:n1].bitcast(FP8X4),
+                    rhs_scale=xs_pick[:, n0:n1],
+                    start=True,
+                    stop=True,
+                )
             nc.scalar.activation(y[t][:, lo:hi], acc[:, 0 : hi - lo], ACT.Relu, bias=b1_sb[:, t : t + 1])
 
         z_bf = sb.tile([P, U * PACK], BF16, name="z_bf", align_bytes=64)

@@ -22,7 +22,8 @@ BANK = 512
 HALF = S // 2
 FIRST = 128
 CHUNKS = (128, 256, 256, 256, 128)
-SPLIT = 768
+SPLIT = 640
+BACK = 768
 
 
 def tile_picked_sae8_relu_po_kernel(
@@ -41,29 +42,30 @@ def tile_picked_sae8_relu_po_kernel(
         held_sb = lists.tile([P, S // 16], U16, name="held_sb")
         w1_raw = sb.tile([P, PACK, H], F32, name="w1_raw", tag="raw", align_bytes=64)
         x_tab = sb.tile([P, T], U32, name="x_tab", align_bytes=64)
-        xs_tab = sb.tile([P, T], U8, name="xs_tab", align_bytes=64)
+        xs_tab = sb.tile([P, T], U8, name="xs_tab", tag="table", align_bytes=64)
         b1_sb = sb.tile([P, PACK], F32, name="b1_sb")
         z = [sb.tile([P, U], F32, name=f"z{t}", align_bytes=64) for t in range(2)]
-        xs_rows = sb.tile([P, T], U8, name="xs_rows", align_bytes=64)
-
-        nc.vector.memset(xs_tab[:].bitcast(I32), 0)
+        xs_pick = sb.tile([P, S], U8, name="xs_pick", align_bytes=64)
+        xs_rows = sb.tile([P, S], U8, name="xs_rows", align_bytes=64)
 
         nc.sync.dma_start(offs_sb[:], offs)
-        for q in range(4):
-            queue = nc.sync if q == 0 else nc.scalar
-            queue.dma_start(xs_rows[32 * q : 32 * q + 4, :].bitcast(I32), x_scales[0, 4 * q : 4 * q + 4, :].bitcast(I32))
+        nc.sync.dma_start(xs_tab[112:128, :].bitcast(I32), x_scales[0].bitcast(I32))
         nc.sync.dma_start(w1_raw[:], w1.rearrange("(p j) c -> p j c", j=PACK))
+        nc.sync.dma_start(x_tab[:].bitcast(I32), x_words[0].rearrange("p c r -> p (c r)").bitcast(I32))
         nc.sync.dma_start(held_sb[:], held)
         nc.sync.dma_start(b1_sb[:], b1.rearrange("(p t) o -> p (t o)", t=PACK))
-        nc.sync.dma_start(x_tab[:].bitcast(I32), x_words[0].rearrange("p c r -> p (c r)").bitcast(I32))
 
-        for t in range(2):
-            nc.vector.memset(z[t][:], 0.0)
-
+        warm = sb.tile([P, 8], F32, name="warm")
+        nc.vector.memset(z[0][:], 0.0)
+        nc.scalar.activation(warm[:], z[0][:, 0:8], ACT.Relu)
+        nc.vector.memset(xs_tab[0:112, :].bitcast(I32), 0)
+        nc.vector.memset(xs_pick[:].bitcast(I32), 0)
+        nc.vector.tensor_copy(xs_rows[:], xs_tab[:].indirect(offs_sb[:]))
         for q in range(4):
-            nc.vector.tensor_copy(xs_tab[32 * q : 32 * q + 4, :].bitcast(I32), xs_rows[32 * q : 32 * q + 4, :].bitcast(I32))
-        xs_pick = sb.tile([P, S], U8, name="xs_pick", align_bytes=64)
-        nc.vector.tensor_copy(xs_pick[:], xs_tab[:].indirect(offs_sb[:]))
+            nc.scalar.dma_start(xs_pick[32 * q : 32 * q + 4, :].bitcast(I32), xs_rows[112 + 4 * q : 116 + 4 * q, :].bitcast(I32))
+        nc.vector.memset(z[1][:], 0.0)
+        z.append(sb.tile([P, U], F32, name="z2", tag="table", align_bytes=64))
+        nc.vector.memset(z[2][:], 0.0)
 
         w1_src = w1_raw[:].rearrange("p j (m t) -> p m j t", t=PACK)
         w1_codes, w1_scales = [], []
@@ -71,7 +73,10 @@ def tile_picked_sae8_relu_po_kernel(
             grouped = sb.tile([P, 2, P, PACK], BF16, name=f"w1_bf{h}", tag=f"stage{h}", align_bytes=64)
             dst = grouped[:].rearrange("p t m j -> p m j t")
             src = w1_src[:, :, :, 2 * h : 2 * h + 2]
-            nc.scalar.copy(dst, src)
+            if h == 0:
+                nc.vector.tensor_copy(dst, src)
+            else:
+                nc.scalar.copy(dst, src)
             codes = sb.tile([P, 2 * P], U32, name=f"w1_codes{h}", align_bytes=64)
             scales = sb.tile([P, 2 * P], U8, name=f"w1_scales{h}", align_bytes=64)
             nc.vector.quantize_mx(codes[:].bitcast(FP8X4), scales[:], grouped[:].rearrange("p t m j -> p (t m j)"))
@@ -88,8 +93,8 @@ def tile_picked_sae8_relu_po_kernel(
         w2_raw = sb.tile([P, 2 * N], U8, name="w2_raw", tag="raw", align_bytes=64)
         w2s_raw = sb.tile([P, N], U8, name="w2s_raw", tag="stage0", align_bytes=64)
         w2_deal = sb.tile([P, 2 * N], U8, name="w2_deal", align_bytes=64)
-        z.append(sb.tile([P, U], F32, name="z2", tag="stage1", align_bytes=64))
-        nc.gpsimd.memset(z[2][:], 0.0)
+        z.append(sb.tile([P, U], F32, name="z3", tag="stage1", align_bytes=64))
+        nc.gpsimd.memset(z[3][:], 0.0)
         w2s_deal = sb.tile([P, N], U8, name="w2s_deal", align_bytes=64)
         nc.sync.dma_start(w2_raw[:].bitcast(I32), w2_words[0].bitcast(I32))
         nc.gpsimd.memset(w2s_raw[:].bitcast(I32), 0)
@@ -128,18 +133,15 @@ def tile_picked_sae8_relu_po_kernel(
         z_slots = z_bf[:].rearrange("p (w t) -> p w t", t=PACK)
         for t, lo, hi in pieces:
             nc.vector.tensor_copy(z[t][:].indirect(held_sb[:, lo // 16 : hi // 16]), y[t][:, lo:hi])
-            if hi == S and t == 0:
-                z.append(sb.tile([P, U], F32, name="z3", tag="y0", align_bytes=64))
-                nc.gpsimd.memset(z[3][:], 0.0)
             if hi == S and t < PACK - 2:
-                nc.scalar.copy(z_slots[:, 0:SPLIT, t], z[t][:, 0:SPLIT])
-                nc.gpsimd.tensor_scalar(z_slots[:, SPLIT:U, t], z[t][:, SPLIT:U], 1.0, 0.0, op0=ALU.mult, op1=ALU.add)
+                nc.scalar.copy(z_slots[:, 0:BACK, t], z[t][:, 0:BACK])
+                nc.gpsimd.tensor_scalar(z_slots[:, BACK:U, t], z[t][:, BACK:U], 1.0, 0.0, op0=ALU.mult, op1=ALU.add)
             if t == PACK - 2:
-                for w0 in range(0, SPLIT, SPLIT // 2):
-                    w1_ = w0 + SPLIT // 2
-                    nc.scalar.copy(z_slots[:, w0:w1_, t:PACK], z[t][:, w0:w1_].unsqueeze(2).to_broadcast([P, SPLIT // 2, 2]))
+                for w0, w1_ in ((0, starts[2]), (starts[2], SPLIT)):
+                    nc.scalar.copy(z_slots[:, w0:w1_, t:PACK], z[t][:, w0:w1_].unsqueeze(2).to_broadcast([P, w1_ - w0, 2]))
+                nc.scalar.copy(z_slots[:, SPLIT:BACK, t], z[t][:, SPLIT:BACK])
                 nc.gpsimd.tensor_scalar(
-                    z_slots[:, SPLIT:U, t:PACK], z[t][:, SPLIT:U].unsqueeze(2).to_broadcast([P, U - SPLIT, 2]), 1.0, 0.0, op0=ALU.mult, op1=ALU.add
+                    z_slots[:, BACK:U, t:PACK], z[t][:, BACK:U].unsqueeze(2).to_broadcast([P, U - BACK, 2]), 1.0, 0.0, op0=ALU.mult, op1=ALU.add
                 )
 
         nc.scalar.copy(z_slots[:, SPLIT:U, PACK - 1], z[PACK - 1][:, SPLIT:U])
@@ -174,7 +176,7 @@ def tile_picked_sae8_relu_po_kernel(
                     stop=True,
                 )
                 nc.scalar.activation(res[c][:, t, :], acc[:, 0:n], ACT.Identity, bias=b2_sb[:, t : t + 1])
-                planes = 2 if c < 2 else PACK
+                planes = PACK if n == P else 2
                 if (t + 1) % planes == 0:
                     nc.sync.dma_start(out_rows[:, t + 1 - planes : t + 1, starts[c] : starts[c] + n], res[c][:, t + 1 - planes : t + 1, :])
 
@@ -187,8 +189,8 @@ def tile_picked_sae8_relu_po_kernel(
         def hand_on(c):
             cols = slice(starts[c], starts[c] + CHUNKS[c])
             nc.vector.quantize_mx(out_words[:, cols].bitcast(FP8X4), out_scales[:, cols], res_bf[c][:].rearrange("p n t -> p (n t)"))
-            if c in (1, 3, last):
-                stored = slice({1: 0, 3: starts[2], last: starts[last]}[c], starts[c] + CHUNKS[c])
+            if c in (2, last):
+                stored = slice(0 if c == 2 else starts[3], starts[c] + CHUNKS[c])
                 nc.sync.dma_start(out_1_rows[:, stored], out_words[:, stored].bitcast(I32))
 
         for c in range(len(CHUNKS)):

@@ -21,7 +21,7 @@ PACK = 4
 BANK = 512
 HALF = S // 2
 FIRST = 128
-CHUNKS = (128, 256, 256, 256, 128)
+CHUNKS = (128, 128, 256, 256, 128, 128)
 SPLIT = 640
 BACK = 768
 
@@ -53,7 +53,7 @@ def tile_picked_sae8_relu_po_kernel(
         nc.sync.dma_start(w1_raw[:], w1.rearrange("(p j) c -> p j c", j=PACK))
         nc.sync.dma_start(x_tab[:].bitcast(I32), x_words[0].rearrange("p c r -> p (c r)").bitcast(I32))
         nc.sync.dma_start(held_sb[:], held)
-        nc.sync.dma_start(b1_sb[:], b1.rearrange("(p t) o -> p (t o)", t=PACK))
+        nc.scalar.dma_start(b1_sb[:], b1.rearrange("(p t) o -> p (t o)", t=PACK))
 
         warm = sb.tile([P, 8], F32, name="warm")
         nc.vector.memset(z[0][:], 0.0)
@@ -176,7 +176,7 @@ def tile_picked_sae8_relu_po_kernel(
                     stop=True,
                 )
                 nc.scalar.activation(res[c][:, t, :], acc[:, 0:n], ACT.Identity, bias=b2_sb[:, t : t + 1])
-                planes = PACK if n == P else 2
+                planes = PACK if n == P and c > 0 else 2
                 if (t + 1) % planes == 0:
                     nc.sync.dma_start(out_rows[:, t + 1 - planes : t + 1, starts[c] : starts[c] + n], res[c][:, t + 1 - planes : t + 1, :])
 

@@ -21,7 +21,7 @@ PACK = 4
 BANK = 512
 HALF = S // 2
 FIRST = 128
-CHUNKS = (128, 128, 256, 256, 128, 128)
+WIDE = 256
 SPLIT = 640
 BACK = 768
 
@@ -30,8 +30,6 @@ def tile_picked_sae8_relu_po_kernel(
     tc, x_words, x_scales, w1, b1, w2_words, w2_scales, b2, offs, held, out_0, out_1, out_2
 ):
     nc = tc.nc
-    starts = [sum(CHUNKS[:c]) for c in range(len(CHUNKS))]
-    last = len(CHUNKS) - 1
 
     with ExitStack() as ctx:
         lists = ctx.enter_context(tc.tile_pool(name="lists", bufs=1))
@@ -53,7 +51,7 @@ def tile_picked_sae8_relu_po_kernel(
         nc.sync.dma_start(w1_raw[:], w1.rearrange("(p j) c -> p j c", j=PACK))
         nc.sync.dma_start(x_tab[:].bitcast(I32), x_words[0].rearrange("p c r -> p (c r)").bitcast(I32))
         nc.sync.dma_start(held_sb[:], held)
-        nc.scalar.dma_start(b1_sb[:], b1.rearrange("(p t) o -> p (t o)", t=PACK))
+        nc.sync.dma_start(b1_sb[:], b1.rearrange("(p t) o -> p (t o)", t=PACK))
 
         warm = sb.tile([P, 8], F32, name="warm")
         nc.vector.memset(z[0][:], 0.0)
@@ -137,7 +135,7 @@ def tile_picked_sae8_relu_po_kernel(
                 nc.scalar.copy(z_slots[:, 0:BACK, t], z[t][:, 0:BACK])
                 nc.gpsimd.tensor_scalar(z_slots[:, BACK:U, t], z[t][:, BACK:U], 1.0, 0.0, op0=ALU.mult, op1=ALU.add)
             if t == PACK - 2:
-                for w0, w1_ in ((0, starts[2]), (starts[2], SPLIT)):
+                for w0, w1_ in ((0, WIDE), (WIDE, SPLIT)):
                     nc.scalar.copy(z_slots[:, w0:w1_, t:PACK], z[t][:, w0:w1_].unsqueeze(2).to_broadcast([P, w1_ - w0, 2]))
                 nc.scalar.copy(z_slots[:, SPLIT:BACK, t], z[t][:, SPLIT:BACK])
                 nc.gpsimd.tensor_scalar(
@@ -151,57 +149,68 @@ def tile_picked_sae8_relu_po_kernel(
         out_rows = out_0.rearrange("(p t) w -> p t w", t=PACK)
         out_1_rows = out_1[0].rearrange("p c r -> p (c r)").bitcast(I32)
 
-        z_codes = [sb.tile([P, n], U32, name=f"z_codes{c}", align_bytes=64) for c, n in enumerate(CHUNKS)]
-        z_scales = [sb.tile([P, n], U8, name=f"z_scales{c}", align_bytes=64) for c, n in enumerate(CHUNKS)]
-        res = [sb.tile([P, PACK, n], F32, name=f"res{c}", align_bytes=64) for c, n in enumerate(CHUNKS)]
-        res_bf = [sb.tile([P, n, PACK], BF16, name=f"res_bf{c}", align_bytes=64) for c, n in enumerate(CHUNKS)]
+        stretches = U // WIDE
+        z_codes = sb.tile([P, U], U32, name="z_codes", align_bytes=64)
+        z_scales = sb.tile([P, U], U8, name="z_scales", align_bytes=64)
+        res = [sb.tile([P, PACK, WIDE], F32, name=f"res{r}", align_bytes=64) for r in range(stretches)]
+        res_bf = sb.tile([P, U, PACK], BF16, name="res_bf", align_bytes=64)
+        banks_used = []
 
-        def last_plane(c):
-            cols = slice(starts[c], min(starts[c] + CHUNKS[c], SPLIT))
-            nc.vector.tensor_copy(z_slots[:, cols, PACK - 1], z[PACK - 1][:, cols])
+        def halves(r):
+            return [(r * WIDE, r * WIDE + P), (r * WIDE + P, (r + 1) * WIDE)]
 
-        def decode(c):
-            n = CHUNKS[c]
-            nc.vector.quantize_mx(z_codes[c][:].bitcast(FP8X4), z_scales[c][:], z_bf[:, PACK * starts[c] : PACK * (starts[c] + n)])
-            for t in range(PACK):
-                bank = (PACK * c + t) % 8
-                acc = psum.tile([P, BANK], F32, name=f"acc2_{c}_{t}", tag=f"bank{bank}")
-                nc.tensor.matmul_mx(
-                    out=acc[:, 0:n],
-                    lhsT=w2_deal[:, 2 * P * t : 2 * P * (t + 1)].bitcast(FP4X4),
-                    lhsT_scale=w2s_deal[:, P * t : P * (t + 1)],
-                    rhs=z_codes[c][:].bitcast(FP8X4),
-                    rhs_scale=z_scales[c][:],
-                    start=True,
-                    stop=True,
-                )
-                nc.scalar.activation(res[c][:, t, :], acc[:, 0:n], ACT.Identity, bias=b2_sb[:, t : t + 1])
-                planes = PACK if n == P and c > 0 else 2
-                if (t + 1) % planes == 0:
-                    nc.sync.dma_start(out_rows[:, t + 1 - planes : t + 1, starts[c] : starts[c] + n], res[c][:, t + 1 - planes : t + 1, :])
+        def whole(r):
+            return [(r * WIDE, (r + 1) * WIDE)]
 
-        def round_result(c):
+        def product(t, lo, hi):
+            acc = psum.tile([P, BANK], F32, name=f"acc2_{lo}_{t}", tag=f"bank{len(banks_used) % 8}")
+            banks_used.append(t)
+            nc.tensor.matmul_mx(
+                out=acc[:, 0 : hi - lo],
+                lhsT=w2_deal[:, 2 * P * t : 2 * P * (t + 1)].bitcast(FP4X4),
+                lhsT_scale=w2s_deal[:, P * t : P * (t + 1)],
+                rhs=z_codes[:, lo:hi].bitcast(FP8X4),
+                rhs_scale=z_scales[:, lo:hi],
+                start=True,
+                stop=True,
+            )
+            return acc
+
+        def decode(r):
+            for lo, hi in halves(r) if r == 0 else whole(r):
+                if lo < SPLIT:
+                    nc.vector.tensor_copy(z_slots[:, lo : min(hi, SPLIT), PACK - 1], z[PACK - 1][:, lo : min(hi, SPLIT)])
+                nc.vector.quantize_mx(z_codes[:, lo:hi].bitcast(FP8X4), z_scales[:, lo:hi], z_bf[:, PACK * lo : PACK * hi])
+            for t0 in range(0, PACK, 2):
+                pair = (t0, t0 + 1)
+                wide = {} if r == 0 else {t: product(t, r * WIDE, (r + 1) * WIDE) for t in pair}
+                for lo, hi in whole(r) if 0 < r < stretches - 1 else halves(r):
+                    cols = slice(lo - r * WIDE, hi - r * WIDE)
+                    for t in pair:
+                        sums = product(t, lo, hi)[:, 0:P] if r == 0 else wide[t][:, cols]
+                        nc.scalar.activation(res[r][:, t, cols], sums, ACT.Identity, bias=b2_sb[:, t : t + 1])
+                nc.sync.dma_start(out_rows[:, t0 : t0 + 2, r * WIDE : (r + 1) * WIDE], res[r][:, t0 : t0 + 2, :])
+
+        def round_result(lo, hi):
+            r = lo // WIDE
             nc.vector.tensor_copy(
-                res_bf[c][:].rearrange("p (g i) t -> p g t i", i=4),
-                res[c][:].rearrange("p t (g i) -> p g t i", i=4),
+                res_bf[:, lo:hi, :].rearrange("p (g i) t -> p g t i", i=4),
+                res[r][:, :, lo - r * WIDE : hi - r * WIDE].rearrange("p t (g i) -> p g t i", i=4),
             )
 
-        def hand_on(c):
-            cols = slice(starts[c], starts[c] + CHUNKS[c])
-            nc.vector.quantize_mx(out_words[:, cols].bitcast(FP8X4), out_scales[:, cols], res_bf[c][:].rearrange("p n t -> p (n t)"))
-            if c in (2, last):
-                stored = slice(0 if c == 2 else starts[3], starts[c] + CHUNKS[c])
-                nc.sync.dma_start(out_1_rows[:, stored], out_words[:, stored].bitcast(I32))
+        def hand_on(lo, hi):
+            nc.vector.quantize_mx(out_words[:, lo:hi].bitcast(FP8X4), out_scales[:, lo:hi], res_bf[:, lo:hi, :].rearrange("p n t -> p (n t)"))
+            if hi % (U // 2) == 0:
+                nc.sync.dma_start(out_1_rows[:, hi - U // 2 : hi], out_words[:, hi - U // 2 : hi].bitcast(I32))
 
-        for c in range(len(CHUNKS)):
-            if starts[c] < SPLIT:
-                last_plane(c)
-            decode(c)
-        round_result(0)
-        for c in range(len(CHUNKS)):
-            if c < last:
-                round_result(c + 1)
-            hand_on(c)
+        for r in range(stretches):
+            decode(r)
+        spans = [span for r in range(stretches - 1) for span in whole(r)] + halves(stretches - 1)
+        round_result(*spans[0])
+        for i, span in enumerate(spans):
+            if i + 1 < len(spans):
+                round_result(*spans[i + 1])
+            hand_on(*span)
         for q in range(4):
             queue = nc.sync if q % 2 == 0 else nc.scalar
             queue.dma_start(out_2[0, 4 * q : 4 * q + 4, :].bitcast(I32), out_scales[32 * q : 32 * q + 4, :].bitcast(I32))

@@ -18,7 +18,11 @@ ALU = mybir.AluOpType
 
 P = 128
 PACK = 4
+GROUP = 16
+QUADRANT = 32
+SCALE_ROWS = 16
 BANK = 512
+BANKS = 8
 HALF = S // 2
 FIRST = 128
 WIDE = 256
@@ -31,23 +35,27 @@ def tile_picked_sae8_relu_po_kernel(
 ):
     nc = tc.nc
 
+    def quadrant_rows(q):
+        return slice(QUADRANT * q, QUADRANT * q + 4)
+
     with ExitStack() as ctx:
         lists = ctx.enter_context(tc.tile_pool(name="lists", bufs=1))
         sb = ctx.enter_context(tc.tile_pool(name="sb", bufs=1))
         psum = ctx.enter_context(tc.psum_pool(name="psum", bufs=1))
 
-        offs_sb = lists.tile([P, S // 16], U16, name="offs_sb")
-        held_sb = lists.tile([P, S // 16], U16, name="held_sb")
+        offs_sb = lists.tile([P, S // GROUP], U16, name="offs_sb")
+        held_sb = lists.tile([P, S // GROUP], U16, name="held_sb")
         w1_raw = sb.tile([P, PACK, H], F32, name="w1_raw", tag="raw", align_bytes=64)
         x_tab = sb.tile([P, T], U32, name="x_tab", align_bytes=64)
-        xs_tab = sb.tile([P, T], U8, name="xs_tab", tag="table", align_bytes=64)
+        xs_tab = sb.tile([P, T], U8, name="xs_tab", align_bytes=64)
         b1_sb = sb.tile([P, PACK], F32, name="b1_sb")
         z = [sb.tile([P, U], F32, name=f"z{t}", align_bytes=64) for t in range(2)]
         xs_pick = sb.tile([P, S], U8, name="xs_pick", align_bytes=64)
         xs_rows = sb.tile([P, S], U8, name="xs_rows", align_bytes=64)
 
+        landing = P - SCALE_ROWS
         nc.sync.dma_start(offs_sb[:], offs)
-        nc.sync.dma_start(xs_tab[112:128, :].bitcast(I32), x_scales[0].bitcast(I32))
+        nc.sync.dma_start(xs_tab[landing:P, :].bitcast(I32), x_scales[0].bitcast(I32))
         nc.sync.dma_start(w1_raw[:], w1.rearrange("(p j) c -> p j c", j=PACK))
         nc.sync.dma_start(x_tab[:].bitcast(I32), x_words[0].rearrange("p c r -> p (c r)").bitcast(I32))
         nc.sync.dma_start(held_sb[:], held)
@@ -56,25 +64,19 @@ def tile_picked_sae8_relu_po_kernel(
         warm = sb.tile([P, 8], F32, name="warm")
         nc.vector.memset(z[0][:], 0.0)
         nc.scalar.activation(warm[:], z[0][:, 0:8], ACT.Relu)
-        nc.vector.memset(xs_tab[0:112, :].bitcast(I32), 0)
+
+        nc.vector.memset(xs_tab[0:landing, :].bitcast(I32), 0)
         nc.vector.memset(xs_pick[:].bitcast(I32), 0)
         nc.vector.tensor_copy(xs_rows[:], xs_tab[:].indirect(offs_sb[:]))
         for q in range(4):
-            nc.scalar.dma_start(xs_pick[32 * q : 32 * q + 4, :].bitcast(I32), xs_rows[112 + 4 * q : 116 + 4 * q, :].bitcast(I32))
+            nc.scalar.dma_start(xs_pick[quadrant_rows(q), :].bitcast(I32), xs_rows[landing + 4 * q : landing + 4 * q + 4, :].bitcast(I32))
         nc.vector.memset(z[1][:], 0.0)
-        z.append(sb.tile([P, U], F32, name="z2", tag="table", align_bytes=64))
-        nc.vector.memset(z[2][:], 0.0)
 
         w1_src = w1_raw[:].rearrange("p j (m t) -> p m j t", t=PACK)
         w1_codes, w1_scales = [], []
         for h in range(2):
             grouped = sb.tile([P, 2, P, PACK], BF16, name=f"w1_bf{h}", tag=f"stage{h}", align_bytes=64)
-            dst = grouped[:].rearrange("p t m j -> p m j t")
-            src = w1_src[:, :, :, 2 * h : 2 * h + 2]
-            if h == 0:
-                nc.vector.tensor_copy(dst, src)
-            else:
-                nc.scalar.copy(dst, src)
+            nc.scalar.copy(grouped[:].rearrange("p t m j -> p m j t"), w1_src[:, :, :, 2 * h : 2 * h + 2])
             codes = sb.tile([P, 2 * P], U32, name=f"w1_codes{h}", align_bytes=64)
             scales = sb.tile([P, 2 * P], U8, name=f"w1_scales{h}", align_bytes=64)
             nc.vector.quantize_mx(codes[:].bitcast(FP8X4), scales[:], grouped[:].rearrange("p t m j -> p (t m j)"))
@@ -85,19 +87,19 @@ def tile_picked_sae8_relu_po_kernel(
         for h in range(2):
             nc.vector.tensor_copy(
                 x_pick[:, h * HALF : (h + 1) * HALF],
-                x_tab[:].indirect(offs_sb[:, h * HALF // 16 : (h + 1) * HALF // 16]),
+                x_tab[:].indirect(offs_sb[:, h * HALF // GROUP : (h + 1) * HALF // GROUP]),
             )
 
         w2_raw = sb.tile([P, 2 * N], U8, name="w2_raw", tag="raw", align_bytes=64)
         w2s_raw = sb.tile([P, N], U8, name="w2s_raw", tag="stage0", align_bytes=64)
         w2_deal = sb.tile([P, 2 * N], U8, name="w2_deal", align_bytes=64)
-        z.append(sb.tile([P, U], F32, name="z3", tag="stage1", align_bytes=64))
-        nc.gpsimd.memset(z[3][:], 0.0)
+        z.append(sb.tile([P, U], F32, name="z2", tag="stage1", align_bytes=64))
+        nc.gpsimd.memset(z[2][:], 0.0)
         w2s_deal = sb.tile([P, N], U8, name="w2s_deal", align_bytes=64)
         nc.sync.dma_start(w2_raw[:].bitcast(I32), w2_words[0].bitcast(I32))
         nc.gpsimd.memset(w2s_raw[:].bitcast(I32), 0)
         for q in range(4):
-            nc.sync.dma_start(w2s_raw[32 * q : 32 * q + 4, :].bitcast(I32), w2_scales[0, 4 * q : 4 * q + 4, :].bitcast(I32))
+            nc.sync.dma_start(w2s_raw[quadrant_rows(q), :].bitcast(I32), w2_scales[0, 4 * q : 4 * q + 4, :].bitcast(I32))
         nc.gpsimd.tensor_copy(
             w2_deal[:].rearrange("p (t m b) -> p t m b", t=PACK, b=2),
             w2_raw[:].rearrange("p (m t b) -> p t m b", t=PACK, b=2),
@@ -113,13 +115,13 @@ def tile_picked_sae8_relu_po_kernel(
         pieces = [(0, 0, FIRST), (1, 0, HALF), (0, FIRST, S), (1, HALF, S), (2, 0, S), (3, 0, S)]
         for i, (t, lo, hi) in enumerate(pieces):
             acc = psum.tile([P, BANK], F32, name=f"acc1_{i}", tag=f"bank{i}")
-            cols = slice((t % 2) * P, (t % 2 + 1) * P)
+            w1_cols = slice((t % 2) * P, (t % 2 + 1) * P)
             cuts = [lo, HALF, hi] if lo == FIRST else [lo, hi]
             for n0, n1 in zip(cuts, cuts[1:]):
                 nc.tensor.matmul_mx(
                     out=acc[:, n0 - lo : n1 - lo],
-                    lhsT=w1_codes[t // 2][:, cols].bitcast(FP8X4),
-                    lhsT_scale=w1_scales[t // 2][:, cols],
+                    lhsT=w1_codes[t // 2][:, w1_cols].bitcast(FP8X4),
+                    lhsT_scale=w1_scales[t // 2][:, w1_cols],
                     rhs=x_pick[:, n0:n1].bitcast(FP8X4),
                     rhs_scale=xs_pick[:, n0:n1],
                     start=True,
@@ -129,18 +131,23 @@ def tile_picked_sae8_relu_po_kernel(
 
         z_bf = sb.tile([P, U * PACK], BF16, name="z_bf", align_bytes=64)
         z_slots = z_bf[:].rearrange("p (w t) -> p w t", t=PACK)
+
+        def both_slots(t, lo, hi):
+            return z[t][:, lo:hi].unsqueeze(2).to_broadcast([P, hi - lo, 2])
+
         for t, lo, hi in pieces:
-            nc.vector.tensor_copy(z[t][:].indirect(held_sb[:, lo // 16 : hi // 16]), y[t][:, lo:hi])
-            if hi == S and t < PACK - 2:
+            nc.vector.tensor_copy(z[t][:].indirect(held_sb[:, lo // GROUP : hi // GROUP]), y[t][:, lo:hi])
+            if hi == S and t == 0:
+                z.append(sb.tile([P, U], F32, name="z3", tag="y0", align_bytes=64))
+                nc.gpsimd.memset(z[3][:], 0.0)
+            if hi == S and t < 2:
                 nc.scalar.copy(z_slots[:, 0:BACK, t], z[t][:, 0:BACK])
                 nc.gpsimd.tensor_scalar(z_slots[:, BACK:U, t], z[t][:, BACK:U], 1.0, 0.0, op0=ALU.mult, op1=ALU.add)
-            if t == PACK - 2:
-                for w0, w1_ in ((0, WIDE), (WIDE, SPLIT)):
-                    nc.scalar.copy(z_slots[:, w0:w1_, t:PACK], z[t][:, w0:w1_].unsqueeze(2).to_broadcast([P, w1_ - w0, 2]))
+            if t == 2:
+                for w_lo, w_hi in ((0, WIDE), (WIDE, SPLIT)):
+                    nc.scalar.copy(z_slots[:, w_lo:w_hi, t:PACK], both_slots(t, w_lo, w_hi))
                 nc.scalar.copy(z_slots[:, SPLIT:BACK, t], z[t][:, SPLIT:BACK])
-                nc.gpsimd.tensor_scalar(
-                    z_slots[:, BACK:U, t:PACK], z[t][:, BACK:U].unsqueeze(2).to_broadcast([P, U - BACK, 2]), 1.0, 0.0, op0=ALU.mult, op1=ALU.add
-                )
+                nc.gpsimd.tensor_scalar(z_slots[:, BACK:U, t:PACK], both_slots(t, BACK, U), 1.0, 0.0, op0=ALU.mult, op1=ALU.add)
 
         nc.scalar.copy(z_slots[:, SPLIT:U, PACK - 1], z[PACK - 1][:, SPLIT:U])
 
@@ -150,21 +157,27 @@ def tile_picked_sae8_relu_po_kernel(
         out_1_rows = out_1[0].rearrange("p c r -> p (c r)").bitcast(I32)
 
         stretches = U // WIDE
+        last = stretches - 1
         z_codes = sb.tile([P, U], U32, name="z_codes", align_bytes=64)
         z_scales = sb.tile([P, U], U8, name="z_scales", align_bytes=64)
         res = [sb.tile([P, PACK, WIDE], F32, name=f"res{r}", align_bytes=64) for r in range(stretches)]
         res_bf = sb.tile([P, U, PACK], BF16, name="res_bf", align_bytes=64)
-        banks_used = []
+        products = []
 
         def halves(r):
-            return [(r * WIDE, r * WIDE + P), (r * WIDE + P, (r + 1) * WIDE)]
+            return [(r * WIDE, r * WIDE + WIDE // 2), (r * WIDE + WIDE // 2, (r + 1) * WIDE)]
 
         def whole(r):
             return [(r * WIDE, (r + 1) * WIDE)]
 
+        def quantise_z(lo, hi):
+            laid = slice(lo, min(hi, SPLIT))
+            nc.vector.tensor_copy(z_slots[:, laid, PACK - 1], z[PACK - 1][:, laid])
+            nc.vector.quantize_mx(z_codes[:, lo:hi].bitcast(FP8X4), z_scales[:, lo:hi], z_bf[:, PACK * lo : PACK * hi])
+
         def product(t, lo, hi):
-            acc = psum.tile([P, BANK], F32, name=f"acc2_{lo}_{t}", tag=f"bank{len(banks_used) % 8}")
-            banks_used.append(t)
+            acc = psum.tile([P, BANK], F32, name=f"acc2_{lo}_{t}", tag=f"bank{len(products) % BANKS}")
+            products.append(acc)
             nc.tensor.matmul_mx(
                 out=acc[:, 0 : hi - lo],
                 lhsT=w2_deal[:, 2 * P * t : 2 * P * (t + 1)].bitcast(FP4X4),
@@ -177,18 +190,15 @@ def tile_picked_sae8_relu_po_kernel(
             return acc
 
         def decode(r):
-            for lo, hi in halves(r) if r == 0 else whole(r):
-                if lo < SPLIT:
-                    nc.vector.tensor_copy(z_slots[:, lo : min(hi, SPLIT), PACK - 1], z[PACK - 1][:, lo : min(hi, SPLIT)])
-                nc.vector.quantize_mx(z_codes[:, lo:hi].bitcast(FP8X4), z_scales[:, lo:hi], z_bf[:, PACK * lo : PACK * hi])
             for t0 in range(0, PACK, 2):
                 pair = (t0, t0 + 1)
-                wide = {} if r == 0 else {t: product(t, r * WIDE, (r + 1) * WIDE) for t in pair}
-                for lo, hi in whole(r) if 0 < r < stretches - 1 else halves(r):
-                    cols = slice(lo - r * WIDE, hi - r * WIDE)
+                if r > 0:
+                    banks = {t: product(t, r * WIDE, (r + 1) * WIDE) for t in pair}
+                for lo, hi in halves(r) if r in (0, last) else whole(r):
+                    res_cols = slice(lo - r * WIDE, hi - r * WIDE)
                     for t in pair:
-                        sums = product(t, lo, hi)[:, 0:P] if r == 0 else wide[t][:, cols]
-                        nc.scalar.activation(res[r][:, t, cols], sums, ACT.Identity, bias=b2_sb[:, t : t + 1])
+                        sums = banks[t][:, res_cols] if r > 0 else product(t, lo, hi)[:, 0 : hi - lo]
+                        nc.scalar.activation(res[r][:, t, res_cols], sums, ACT.Identity, bias=b2_sb[:, t : t + 1])
                 nc.sync.dma_start(out_rows[:, t0 : t0 + 2, r * WIDE : (r + 1) * WIDE], res[r][:, t0 : t0 + 2, :])
 
         def round_result(lo, hi):
@@ -203,14 +213,22 @@ def tile_picked_sae8_relu_po_kernel(
             if hi % (U // 2) == 0:
                 nc.sync.dma_start(out_1_rows[:, hi - U // 2 : hi], out_words[:, hi - U // 2 : hi].bitcast(I32))
 
-        for r in range(stretches):
+        for lo, hi in halves(0):
+            quantise_z(lo, hi)
+        decode(0)
+        quantise_z(WIDE, U // 2)
+        decode(1)
+        quantise_z(U // 2, U)
+        for r in range(2, stretches):
             decode(r)
-        spans = [span for r in range(stretches - 1) for span in whole(r)] + halves(stretches - 1)
-        round_result(*spans[0])
-        for i, span in enumerate(spans):
-            if i + 1 < len(spans):
-                round_result(*spans[i + 1])
-            hand_on(*span)
+
+        for r in range(last):
+            round_result(r * WIDE, (r + 1) * WIDE)
+        hand_on(0, U // 2)
+        for lo, hi in halves(last):
+            round_result(lo, hi)
+        for lo, hi in whole(last - 1) + halves(last):
+            hand_on(lo, hi)
         for q in range(4):
             queue = nc.sync if q % 2 == 0 else nc.scalar
-            queue.dma_start(out_2[0, 4 * q : 4 * q + 4, :].bitcast(I32), out_scales[32 * q : 32 * q + 4, :].bitcast(I32))
+            queue.dma_start(out_2[0, 4 * q : 4 * q + 4, :].bitcast(I32), out_scales[quadrant_rows(q), :].bitcast(I32))

@@ -95,7 +95,6 @@ def tile_picked_sae8_relu_po_kernel(
         w2_deal = sb.tile([P, 2 * N], U8, name="w2_deal", align_bytes=64)
         z.append(sb.tile([P, U], F32, name="z2", tag="stage1", align_bytes=64))
         nc.gpsimd.memset(z[2][:], 0.0)
-        w2s_deal = sb.tile([P, N], U8, name="w2s_deal", align_bytes=64)
         nc.sync.dma_start(w2_raw[:].bitcast(I32), w2_words[0].bitcast(I32))
         nc.gpsimd.memset(w2s_raw[:].bitcast(I32), 0)
         for q in range(4):
@@ -104,11 +103,7 @@ def tile_picked_sae8_relu_po_kernel(
             w2_deal[:].rearrange("p (t m b) -> p t m b", t=PACK, b=2),
             w2_raw[:].rearrange("p (m t b) -> p t m b", t=PACK, b=2),
         )
-        nc.gpsimd.tensor_copy(
-            w2s_deal[:].rearrange("p (t m) -> p t m", t=PACK),
-            w2s_raw[:].rearrange("p (m t) -> p t m", t=PACK),
-        )
-        b2_sb = sb.tile([P, PACK], F32, name="b2_sb", tag="stage0", align_bytes=64)
+        b2_sb = sb.tile([P, PACK], F32, name="b2_sb", tag="raw", align_bytes=64)
         nc.sync.dma_start(b2_sb[:], b2.rearrange("(p t) o -> p (t o)", t=PACK))
 
         y = [sb.tile([P, S], F32, name=f"y{t}", tag=f"y{t}", align_bytes=64) for t in range(PACK)]
@@ -148,6 +143,22 @@ def tile_picked_sae8_relu_po_kernel(
                     nc.scalar.copy(z_slots[:, w_lo:w_hi, t:PACK], both_slots(t, w_lo, w_hi))
                 nc.scalar.copy(z_slots[:, SPLIT:BACK, t], z[t][:, SPLIT:BACK])
                 nc.gpsimd.tensor_scalar(z_slots[:, BACK:U, t:PACK], both_slots(t, BACK, U), 1.0, 0.0, op0=ALU.mult, op1=ALU.add)
+                w2s_deal = sb.tile([P, N], U8, name="w2s_deal", tag="y2", align_bytes=64)
+                nc.gpsimd.tensor_copy(
+                    w2s_deal[:].rearrange("p (t m) -> p t m", t=PACK),
+                    w2s_raw[:].rearrange("p (m t) -> p t m", t=PACK),
+                )
+                idle = psum.tile([P, BANK], F32, name="idle", tag="bank7")
+                for rep in range(3):
+                    nc.tensor.matmul_mx(
+                        out=idle[:],
+                        lhsT=w2_deal[:, 0 : 2 * P].bitcast(FP4X4),
+                        lhsT_scale=w2s_deal[:, 0:P],
+                        rhs=x_pick[:].bitcast(FP8X4),
+                        rhs_scale=xs_pick[:],
+                        start=True,
+                        stop=True,
+                    )
 
         nc.scalar.copy(z_slots[:, SPLIT:U, PACK - 1], z[PACK - 1][:, SPLIT:U])
 
@@ -192,12 +203,10 @@ def tile_picked_sae8_relu_po_kernel(
         def decode(r):
             for t0 in range(0, PACK, 2):
                 pair = (t0, t0 + 1)
-                if r > 0:
-                    banks = {t: product(t, r * WIDE, (r + 1) * WIDE) for t in pair}
                 for lo, hi in halves(r) if r in (0, last) else whole(r):
                     res_cols = slice(lo - r * WIDE, hi - r * WIDE)
                     for t in pair:
-                        sums = banks[t][:, res_cols] if r > 0 else product(t, lo, hi)[:, 0 : hi - lo]
+                        sums = product(t, lo, hi)[:, 0 : hi - lo]
                         nc.scalar.activation(res[r][:, t, res_cols], sums, ACT.Identity, bias=b2_sb[:, t : t + 1])
                 nc.sync.dma_start(out_rows[:, t0 : t0 + 2, r * WIDE : (r + 1) * WIDE], res[r][:, t0 : t0 + 2, :])
 

@@ -27,7 +27,7 @@ HALF = S // 2
 FIRST = 128
 WIDE = 256
 SPLIT = 640
-BACK = 768
+BACK = 704
 
 
 def tile_picked_sae8_relu_po_kernel(
@@ -95,6 +95,7 @@ def tile_picked_sae8_relu_po_kernel(
         w2_deal = sb.tile([P, 2 * N], U8, name="w2_deal", align_bytes=64)
         z.append(sb.tile([P, U], F32, name="z2", tag="stage1", align_bytes=64))
         nc.gpsimd.memset(z[2][:], 0.0)
+        w2s_deal = sb.tile([P, N], U8, name="w2s_deal", align_bytes=64)
         nc.sync.dma_start(w2_raw[:].bitcast(I32), w2_words[0].bitcast(I32))
         nc.gpsimd.memset(w2s_raw[:].bitcast(I32), 0)
         for q in range(4):
@@ -103,7 +104,11 @@ def tile_picked_sae8_relu_po_kernel(
             w2_deal[:].rearrange("p (t m b) -> p t m b", t=PACK, b=2),
             w2_raw[:].rearrange("p (m t b) -> p t m b", t=PACK, b=2),
         )
-        b2_sb = sb.tile([P, PACK], F32, name="b2_sb", tag="raw", align_bytes=64)
+        nc.gpsimd.tensor_copy(
+            w2s_deal[:].rearrange("p (t m) -> p t m", t=PACK),
+            w2s_raw[:].rearrange("p (m t) -> p t m", t=PACK),
+        )
+        b2_sb = sb.tile([P, PACK], F32, name="b2_sb", tag="stage0", align_bytes=64)
         nc.sync.dma_start(b2_sb[:], b2.rearrange("(p t) o -> p (t o)", t=PACK))
 
         y = [sb.tile([P, S], F32, name=f"y{t}", tag=f"y{t}", align_bytes=64) for t in range(PACK)]
@@ -124,8 +129,12 @@ def tile_picked_sae8_relu_po_kernel(
                 )
             nc.scalar.activation(y[t][:, lo:hi], acc[:, 0 : hi - lo], ACT.Relu, bias=b1_sb[:, t : t + 1])
 
+        stretches = U // WIDE
+        last = stretches - 1
         z_bf = sb.tile([P, U * PACK], BF16, name="z_bf", align_bytes=64)
-        z_slots = z_bf[:].rearrange("p (w t) -> p w t", t=PACK)
+
+        def slots(lo, hi):
+            return z_bf[:].rearrange("p (w t) -> p w t", t=PACK)[:, lo:hi, :]
 
         def both_slots(t, lo, hi):
             return z[t][:, lo:hi].unsqueeze(2).to_broadcast([P, hi - lo, 2])
@@ -136,108 +145,113 @@ def tile_picked_sae8_relu_po_kernel(
                 z.append(sb.tile([P, U], F32, name="z3", tag="y0", align_bytes=64))
                 nc.gpsimd.memset(z[3][:], 0.0)
             if hi == S and t < 2:
-                nc.scalar.copy(z_slots[:, 0:BACK, t], z[t][:, 0:BACK])
-                nc.gpsimd.tensor_scalar(z_slots[:, BACK:U, t], z[t][:, BACK:U], 1.0, 0.0, op0=ALU.mult, op1=ALU.add)
+                nc.scalar.copy(slots(0, BACK)[:, :, t], z[t][:, 0:BACK])
+                nc.gpsimd.tensor_scalar(slots(BACK, U)[:, :, t], z[t][:, BACK:U], 1.0, 0.0, op0=ALU.mult, op1=ALU.add)
             if t == 2:
-                for w_lo, w_hi in ((0, WIDE), (WIDE, SPLIT)):
-                    nc.scalar.copy(z_slots[:, w_lo:w_hi, t:PACK], both_slots(t, w_lo, w_hi))
-                nc.scalar.copy(z_slots[:, SPLIT:BACK, t], z[t][:, SPLIT:BACK])
-                nc.gpsimd.tensor_scalar(z_slots[:, BACK:U, t:PACK], both_slots(t, BACK, U), 1.0, 0.0, op0=ALU.mult, op1=ALU.add)
-                w2s_deal = sb.tile([P, N], U8, name="w2s_deal", tag="y2", align_bytes=64)
-                nc.gpsimd.tensor_copy(
-                    w2s_deal[:].rearrange("p (t m) -> p t m", t=PACK),
-                    w2s_raw[:].rearrange("p (m t) -> p t m", t=PACK),
-                )
+                nc.scalar.copy(slots(0, WIDE)[:, :, t:PACK], both_slots(t, 0, WIDE))
+                nc.scalar.copy(slots(WIDE, SPLIT)[:, :, t], z[t][:, WIDE:SPLIT])
+                nc.scalar.copy(slots(SPLIT, BACK)[:, :, t:PACK], both_slots(t, SPLIT, BACK))
+                nc.gpsimd.tensor_scalar(slots(BACK, U)[:, :, t:PACK], both_slots(t, BACK, U), 1.0, 0.0, op0=ALU.mult, op1=ALU.add)
+                w2s_late = sb.tile([P, N], U8, name="w2s_late", tag="y2", align_bytes=64)
+                nc.gpsimd.tensor_copy(w2s_late[:].bitcast(I32), w2s_deal[:].bitcast(I32))
                 idle = psum.tile([P, BANK], F32, name="idle", tag="bank7")
                 for rep in range(3):
                     nc.tensor.matmul_mx(
                         out=idle[:],
                         lhsT=w2_deal[:, 0 : 2 * P].bitcast(FP4X4),
-                        lhsT_scale=w2s_deal[:, 0:P],
+                        lhsT_scale=w2s_late[:, 0:P],
                         rhs=x_pick[:].bitcast(FP8X4),
                         rhs_scale=xs_pick[:],
                         start=True,
                         stop=True,
                     )
 
-        nc.scalar.copy(z_slots[:, SPLIT:U, PACK - 1], z[PACK - 1][:, SPLIT:U])
+        for w_lo, w_hi in ((WIDE, 2 * WIDE), (2 * WIDE, SPLIT)):
+            nc.scalar.copy(slots(w_lo, w_hi)[:, :, PACK - 1], z[PACK - 1][:, w_lo:w_hi])
 
         out_words = sb.tile([P, U], U32, name="out_words", align_bytes=64)
         out_scales = sb.tile([P, U], U8, name="out_scales", align_bytes=64)
         out_rows = out_0.rearrange("(p t) w -> p t w", t=PACK)
         out_1_rows = out_1[0].rearrange("p c r -> p (c r)").bitcast(I32)
 
-        stretches = U // WIDE
-        last = stretches - 1
         z_codes = sb.tile([P, U], U32, name="z_codes", align_bytes=64)
         z_scales = sb.tile([P, U], U8, name="z_scales", align_bytes=64)
-        res = [sb.tile([P, PACK, WIDE], F32, name=f"res{r}", align_bytes=64) for r in range(stretches)]
+        res = {}
         res_bf = sb.tile([P, U, PACK], BF16, name="res_bf", align_bytes=64)
         products = []
 
-        def halves(r):
-            return [(r * WIDE, r * WIDE + WIDE // 2), (r * WIDE + WIDE // 2, (r + 1) * WIDE)]
-
-        def whole(r):
-            return [(r * WIDE, (r + 1) * WIDE)]
+        def lay(lo, hi):
+            nc.vector.tensor_copy(slots(lo, hi)[:, :, PACK - 1], z[PACK - 1][:, lo:hi])
 
         def quantise_z(lo, hi):
-            laid = slice(lo, min(hi, SPLIT))
-            nc.vector.tensor_copy(z_slots[:, laid, PACK - 1], z[PACK - 1][:, laid])
             nc.vector.quantize_mx(z_codes[:, lo:hi].bitcast(FP8X4), z_scales[:, lo:hi], z_bf[:, PACK * lo : PACK * hi])
 
-        def product(t, lo, hi):
+        def unit(t, lo, hi, on_vector=False):
+            r = lo // WIDE
             acc = psum.tile([P, BANK], F32, name=f"acc2_{lo}_{t}", tag=f"bank{len(products) % BANKS}")
             products.append(acc)
             nc.tensor.matmul_mx(
                 out=acc[:, 0 : hi - lo],
                 lhsT=w2_deal[:, 2 * P * t : 2 * P * (t + 1)].bitcast(FP4X4),
-                lhsT_scale=w2s_deal[:, P * t : P * (t + 1)],
+                lhsT_scale=w2s_late[:, P * t : P * (t + 1)],
                 rhs=z_codes[:, lo:hi].bitcast(FP8X4),
                 rhs_scale=z_scales[:, lo:hi],
                 start=True,
                 stop=True,
             )
-            return acc
+            cols = slice(lo - r * WIDE, hi - r * WIDE)
+            if on_vector:
+                nc.vector.tensor_scalar(res[r][:, t, cols], acc[:, 0 : hi - lo], b2_sb[:, t : t + 1], None, op0=ALU.add)
+            else:
+                nc.scalar.activation(res[r][:, t, cols], acc[:, 0 : hi - lo], ACT.Identity, bias=b2_sb[:, t : t + 1])
 
-        def decode(r):
-            for t0 in range(0, PACK, 2):
-                pair = (t0, t0 + 1)
-                for lo, hi in halves(r) if r in (0, last) else whole(r):
-                    res_cols = slice(lo - r * WIDE, hi - r * WIDE)
-                    for t in pair:
-                        sums = product(t, lo, hi)[:, 0 : hi - lo]
-                        nc.scalar.activation(res[r][:, t, res_cols], sums, ACT.Identity, bias=b2_sb[:, t : t + 1])
-                nc.sync.dma_start(out_rows[:, t0 : t0 + 2, r * WIDE : (r + 1) * WIDE], res[r][:, t0 : t0 + 2, :])
+        def store(r, t0, t1, queue=nc.sync):
+            queue.dma_start(out_rows[:, t0:t1, r * WIDE : (r + 1) * WIDE], res[r][:, t0:t1, :])
 
-        def round_result(lo, hi):
+        def round_result(lo, hi, engine_copy=nc.vector.tensor_copy):
             r = lo // WIDE
-            nc.vector.tensor_copy(
+            engine_copy(
                 res_bf[:, lo:hi, :].rearrange("p (g i) t -> p g t i", i=4),
                 res[r][:, :, lo - r * WIDE : hi - r * WIDE].rearrange("p t (g i) -> p g t i", i=4),
             )
 
-        def hand_on(lo, hi):
+        def quantise_result(lo, hi):
             nc.vector.quantize_mx(out_words[:, lo:hi].bitcast(FP8X4), out_scales[:, lo:hi], res_bf[:, lo:hi, :].rearrange("p n t -> p (n t)"))
-            if hi % (U // 2) == 0:
-                nc.sync.dma_start(out_1_rows[:, hi - U // 2 : hi], out_words[:, hi - U // 2 : hi].bitcast(I32))
 
-        for lo, hi in halves(0):
-            quantise_z(lo, hi)
-        decode(0)
-        quantise_z(WIDE, U // 2)
-        decode(1)
-        quantise_z(U // 2, U)
-        for r in range(2, stretches):
-            decode(r)
+        def store_words(lo, hi):
+            nc.sync.dma_start(out_1_rows[:, lo:hi], out_words[:, lo:hi].bitcast(I32))
 
-        for r in range(last):
-            round_result(r * WIDE, (r + 1) * WIDE)
-        hand_on(0, U // 2)
-        for lo, hi in halves(last):
-            round_result(lo, hi)
-        for lo, hi in whole(last - 1) + halves(last):
-            hand_on(lo, hi)
+        for r in range(stretches):
+            res[r] = sb.tile([P, PACK, WIDE], F32, name=f"res{r}", align_bytes=64)
+        lay(0, 128)
+        lay(128, 256)
+        quantise_z(0, 128)
+        quantise_z(128, 256)
+        lay(SPLIT, 768)
+        quantise_z(256, 512)
+        lay(768, U)
+        quantise_z(512, 768)
+        quantise_z(768, 1024)
+        for r in range(stretches):
+            lo, hi = r * WIDE, (r + 1) * WIDE
+            for pair in [(0,), (1,), (2, 3)] if r == 0 else [(0, 1), (2, 3)]:
+                for n0, n1 in ((lo, lo + 128), (lo + 128, hi)) if r in (0, last) else ((lo, hi),):
+                    for t in pair:
+                        unit(t, n0, n1, on_vector=(r == 1 and t < 2))
+                if r < last:
+                    store(r, pair[0], pair[-1] + 1)
+        store(last, 0, PACK)
+        round_result(0, 256)
+        round_result(256, 512)
+        round_result(512, 768)
+        quantise_result(0, 512)
+        store_words(0, 512)
+        round_result(768, 896)
+        round_result(896, 1024, nc.scalar.copy)
+        quantise_result(512, 768)
+        quantise_result(768, 896)
+        quantise_result(896, 1024)
+        store_words(512, 1024)
         for q in range(4):
             queue = nc.sync if q % 2 == 0 else nc.scalar
             queue.dma_start(out_2[0, 4 * q : 4 * q + 4, :].bitcast(I32), out_scales[quadrant_rows(q), :].bitcast(I32))

@@ -218,8 +218,8 @@ def tile_picked_sae8_relu_po_kernel(
         def quantise_result(lo, hi):
             nc.vector.quantize_mx(out_words[:, lo:hi].bitcast(FP8X4), out_scales[:, lo:hi], res_bf[:, lo:hi, :].rearrange("p n t -> p (n t)"))
 
-        def store_words(lo, hi):
-            nc.sync.dma_start(out_1_rows[:, lo:hi], out_words[:, lo:hi].bitcast(I32))
+        def store_words(lo, hi, queue=nc.sync):
+            queue.dma_start(out_1_rows[:, lo:hi], out_words[:, lo:hi].bitcast(I32))
 
         for r in range(stretches):
             res[r] = sb.tile([P, PACK, WIDE], F32, name=f"res{r}", align_bytes=64)
@@ -234,13 +234,14 @@ def tile_picked_sae8_relu_po_kernel(
         quantise_z(768, 1024)
         for r in range(stretches):
             lo, hi = r * WIDE, (r + 1) * WIDE
-            for pair in [(0,), (1,), (2, 3)] if r == 0 else [(0, 1), (2, 3)]:
+            for pair in [(0,), (1,), (2,), (3,)] if r == 0 else [(0, 1), (2, 3)]:
                 for n0, n1 in ((lo, lo + 128), (lo + 128, hi)) if r in (0, last) else ((lo, hi),):
                     for t in pair:
-                        unit(t, n0, n1, on_vector=(r == 1 and t < 2))
-                if r < last:
+                        unit(t, n0, n1, on_vector=(r == 1 and t % 2 == 1))
+                if r < 2:
                     store(r, pair[0], pair[-1] + 1)
-        store(last, 0, PACK)
+            if r >= 2:
+                store(r, 0, PACK)
         round_result(0, 256)
         round_result(256, 512)
         round_result(512, 768)
@@ -251,7 +252,7 @@ def tile_picked_sae8_relu_po_kernel(
         quantise_result(512, 768)
         quantise_result(768, 896)
         quantise_result(896, 1024)
-        store_words(512, 1024)
+        store_words(512, 1024, nc.scalar)
         for q in range(4):
             queue = nc.sync if q % 2 == 0 else nc.scalar
             queue.dma_start(out_2[0, 4 * q : 4 * q + 4, :].bitcast(I32), out_scales[quadrant_rows(q), :].bitcast(I32))

@@ -116,7 +116,7 @@ def tile_picked_sae8_relu_po_kernel(
         for i, (t, lo, hi) in enumerate(pieces):
             acc = psum.tile([P, BANK], F32, name=f"acc1_{i}", tag=f"bank{i}")
             w1_cols = slice((t % 2) * P, (t % 2 + 1) * P)
-            cuts = [lo, HALF, hi] if lo == FIRST else [lo, hi]
+            cuts = [lo, HALF, hi] if lo < HALF < hi else [lo, hi]
             for n0, n1 in zip(cuts, cuts[1:]):
                 nc.tensor.matmul_mx(
                     out=acc[:, n0 - lo : n1 - lo],
@@ -186,19 +186,26 @@ def tile_picked_sae8_relu_po_kernel(
         def quantise_z(lo, hi):
             nc.vector.quantize_mx(z_codes[:, lo:hi].bitcast(FP8X4), z_scales[:, lo:hi], z_bf[:, PACK * lo : PACK * hi])
 
+        blocks = [(0, 256), (256, 512), (512, 1024)]
+
+        def block_of(lo):
+            return min(lo // WIDE, 2)
+
         def unit(t, lo, hi, on_vector=False):
-            r = lo // WIDE
+            r = block_of(lo)
             acc = psum.tile([P, BANK], F32, name=f"acc2_{lo}_{t}", tag=f"bank{len(products) % BANKS}")
             products.append(acc)
-            nc.tensor.matmul_mx(
-                out=acc[:, 0 : hi - lo],
-                lhsT=w2_deal[:, 2 * P * t : 2 * P * (t + 1)].bitcast(FP4X4),
-                lhsT_scale=w2s_late[:, P * t : P * (t + 1)],
-                rhs=z_codes[:, lo:hi].bitcast(FP8X4),
-                rhs_scale=z_scales[:, lo:hi],
-                start=True,
-                stop=True,
-            )
+            for n0 in range(lo, hi, WIDE):
+                n1 = min(hi, n0 + WIDE)
+                nc.tensor.matmul_mx(
+                    out=acc[:, n0 - lo : n1 - lo],
+                    lhsT=w2_deal[:, 2 * P * t : 2 * P * (t + 1)].bitcast(FP4X4),
+                    lhsT_scale=w2s_late[:, P * t : P * (t + 1)],
+                    rhs=z_codes[:, n0:n1].bitcast(FP8X4),
+                    rhs_scale=z_scales[:, n0:n1],
+                    start=True,
+                    stop=True,
+                )
             cols = slice(lo - r * WIDE, hi - r * WIDE)
             if on_vector:
                 nc.vector.tensor_scalar(res[r][:, t, cols], acc[:, 0 : hi - lo], b2_sb[:, t : t + 1], None, op0=ALU.add)
@@ -206,10 +213,10 @@ def tile_picked_sae8_relu_po_kernel(
                 nc.scalar.activation(res[r][:, t, cols], acc[:, 0 : hi - lo], ACT.Identity, bias=b2_sb[:, t : t + 1])
 
         def store(r, t0, t1, queue=nc.sync):
-            queue.dma_start(out_rows[:, t0:t1, r * WIDE : (r + 1) * WIDE], res[r][:, t0:t1, :])
+            queue.dma_start(out_rows[:, t0:t1, blocks[r][0] : blocks[r][1]], res[r][:, t0:t1, :])
 
         def round_result(lo, hi, engine_copy=nc.vector.tensor_copy):
-            r = lo // WIDE
+            r = block_of(lo)
             engine_copy(
                 res_bf[:, lo:hi, :].rearrange("p (g i) t -> p g t i", i=4),
                 res[r][:, :, lo - r * WIDE : hi - r * WIDE].rearrange("p t (g i) -> p g t i", i=4),
@@ -221,8 +228,8 @@ def tile_picked_sae8_relu_po_kernel(
         def store_words(lo, hi, queue=nc.sync):
             queue.dma_start(out_1_rows[:, lo:hi], out_words[:, lo:hi].bitcast(I32))
 
-        for r in range(stretches):
-            res[r] = sb.tile([P, PACK, WIDE], F32, name=f"res{r}", align_bytes=64)
+        for r, (lo, hi) in enumerate(blocks):
+            res[r] = sb.tile([P, PACK, hi - lo], F32, name=f"res{r}", align_bytes=64)
         lay(0, 128)
         lay(128, 256)
         quantise_z(0, 128)
@@ -232,16 +239,21 @@ def tile_picked_sae8_relu_po_kernel(
         lay(768, U)
         quantise_z(512, 768)
         quantise_z(768, 1024)
-        for r in range(stretches):
-            lo, hi = r * WIDE, (r + 1) * WIDE
-            for pair in [(0,), (1,), (2,), (3,)] if r == 0 else [(0, 1), (2, 3)]:
-                for n0, n1 in ((lo, lo + 128), (lo + 128, hi)) if r in (0, last) else ((lo, hi),):
-                    for t in pair:
-                        unit(t, n0, n1, on_vector=(r == 1 and t % 2 == 1))
-                if r < 2:
-                    store(r, pair[0], pair[-1] + 1)
-            if r >= 2:
-                store(r, 0, PACK)
+        for t in range(PACK):
+            unit(t, 0, 128)
+            unit(t, 128, 256)
+            store(0, t, t + 1)
+        for t in range(PACK):
+            unit(t, 256, 512, on_vector=t % 2 == 1)
+            if t % 2:
+                store(1, t - 1, t + 1)
+        for t in (0, 1):
+            unit(t, 512, 1024)
+            store(2, t, t + 1)
+        for lo, hi in ((512, 768), (768, 896), (896, 1024)):
+            for t in (2, 3):
+                unit(t, lo, hi)
+        store(2, 2, PACK)
         round_result(0, 256)
         round_result(256, 512)
         round_result(512, 768)

@@ -25,9 +25,12 @@ BANK = 512
 BANKS = 8
 HALF = S // 2
 FIRST = 128
-WIDE = 256
+QUARTER = U // 4
+EIGHTH = U // 8
+MID = U // 2
 SPLIT = 640
 BACK = 704
+WARM_PASSES = 3
 
 
 def tile_picked_sae8_relu_po_kernel(
@@ -108,7 +111,7 @@ def tile_picked_sae8_relu_po_kernel(
             w2s_deal[:].rearrange("p (t m) -> p t m", t=PACK),
             w2s_raw[:].rearrange("p (m t) -> p t m", t=PACK),
         )
-        b2_sb = sb.tile([P, PACK], F32, name="b2_sb", tag="stage0", align_bytes=64)
+        b2_sb = sb.tile([P, PACK], F32, name="b2_sb", tag="raw", align_bytes=64)
         nc.sync.dma_start(b2_sb[:], b2.rearrange("(p t) o -> p (t o)", t=PACK))
 
         y = [sb.tile([P, S], F32, name=f"y{t}", tag=f"y{t}", align_bytes=64) for t in range(PACK)]
@@ -129,12 +132,8 @@ def tile_picked_sae8_relu_po_kernel(
                 )
             nc.scalar.activation(y[t][:, lo:hi], acc[:, 0 : hi - lo], ACT.Relu, bias=b1_sb[:, t : t + 1])
 
-        stretches = U // WIDE
-        last = stretches - 1
         z_bf = sb.tile([P, U * PACK], BF16, name="z_bf", align_bytes=64)
-
-        def slots(lo, hi):
-            return z_bf[:].rearrange("p (w t) -> p w t", t=PACK)[:, lo:hi, :]
+        z_slots = z_bf[:].rearrange("p (w t) -> p w t", t=PACK)
 
         def both_slots(t, lo, hi):
             return z[t][:, lo:hi].unsqueeze(2).to_broadcast([P, hi - lo, 2])
@@ -145,19 +144,19 @@ def tile_picked_sae8_relu_po_kernel(
                 z.append(sb.tile([P, U], F32, name="z3", tag="y0", align_bytes=64))
                 nc.gpsimd.memset(z[3][:], 0.0)
             if hi == S and t < 2:
-                nc.scalar.copy(slots(0, BACK)[:, :, t], z[t][:, 0:BACK])
-                nc.gpsimd.tensor_scalar(slots(BACK, U)[:, :, t], z[t][:, BACK:U], 1.0, 0.0, op0=ALU.mult, op1=ALU.add)
+                nc.scalar.copy(z_slots[:, 0:BACK, t], z[t][:, 0:BACK])
+                nc.gpsimd.tensor_scalar(z_slots[:, BACK:U, t], z[t][:, BACK:U], 1.0, 0.0, op0=ALU.mult, op1=ALU.add)
             if t == 2:
-                nc.scalar.copy(slots(0, WIDE)[:, :, t:PACK], both_slots(t, 0, WIDE))
-                nc.scalar.copy(slots(WIDE, SPLIT)[:, :, t], z[t][:, WIDE:SPLIT])
-                nc.scalar.copy(slots(SPLIT, BACK)[:, :, t:PACK], both_slots(t, SPLIT, BACK))
-                nc.gpsimd.tensor_scalar(slots(BACK, U)[:, :, t:PACK], both_slots(t, BACK, U), 1.0, 0.0, op0=ALU.mult, op1=ALU.add)
+                nc.scalar.copy(z_slots[:, 0:QUARTER, t:PACK], both_slots(t, 0, QUARTER))
+                nc.scalar.copy(z_slots[:, QUARTER:SPLIT, t], z[t][:, QUARTER:SPLIT])
+                nc.scalar.copy(z_slots[:, SPLIT:BACK, t:PACK], both_slots(t, SPLIT, BACK))
+                nc.gpsimd.tensor_scalar(z_slots[:, BACK:U, t:PACK], both_slots(t, BACK, U), 1.0, 0.0, op0=ALU.mult, op1=ALU.add)
                 w2s_late = sb.tile([P, N], U8, name="w2s_late", tag="y2", align_bytes=64)
                 nc.gpsimd.tensor_copy(w2s_late[:].bitcast(I32), w2s_deal[:].bitcast(I32))
-                idle = psum.tile([P, BANK], F32, name="idle", tag="bank7")
-                for rep in range(3):
+                unread = psum.tile([P, BANK], F32, name="unread", tag=f"bank{BANKS - 1}")
+                for rep in range(WARM_PASSES):
                     nc.tensor.matmul_mx(
-                        out=idle[:],
+                        out=unread[:],
                         lhsT=w2_deal[:, 0 : 2 * P].bitcast(FP4X4),
                         lhsT_scale=w2s_late[:, 0:P],
                         rhs=x_pick[:].bitcast(FP8X4),
@@ -166,8 +165,8 @@ def tile_picked_sae8_relu_po_kernel(
                         stop=True,
                     )
 
-        for w_lo, w_hi in ((WIDE, 2 * WIDE), (2 * WIDE, SPLIT)):
-            nc.scalar.copy(slots(w_lo, w_hi)[:, :, PACK - 1], z[PACK - 1][:, w_lo:w_hi])
+        for lo, hi in ((QUARTER, MID), (MID, SPLIT)):
+            nc.scalar.copy(z_slots[:, lo:hi, PACK - 1], z[PACK - 1][:, lo:hi])
 
         out_words = sb.tile([P, U], U32, name="out_words", align_bytes=64)
         out_scales = sb.tile([P, U], U8, name="out_scales", align_bytes=64)
@@ -176,27 +175,25 @@ def tile_picked_sae8_relu_po_kernel(
 
         z_codes = sb.tile([P, U], U32, name="z_codes", align_bytes=64)
         z_scales = sb.tile([P, U], U8, name="z_scales", align_bytes=64)
-        res = {}
         res_bf = sb.tile([P, U, PACK], BF16, name="res_bf", align_bytes=64)
-        products = []
+        res = [sb.tile([P, PACK, MID], F32, name=f"res{r}", align_bytes=64) for r in range(U // MID)]
+        z_cuts = [0, EIGHTH, QUARTER, MID, U - QUARTER, U]
+        banks_used = []
 
-        def lay(lo, hi):
-            nc.vector.tensor_copy(slots(lo, hi)[:, :, PACK - 1], z[PACK - 1][:, lo:hi])
+        def res_cols(t0, t1, lo, hi):
+            return res[lo // MID][:, t0:t1, lo % MID : lo % MID + hi - lo]
+
+        def lay_last_plane(lo, hi):
+            nc.vector.tensor_copy(z_slots[:, lo:hi, PACK - 1], z[PACK - 1][:, lo:hi])
 
         def quantise_z(lo, hi):
             nc.vector.quantize_mx(z_codes[:, lo:hi].bitcast(FP8X4), z_scales[:, lo:hi], z_bf[:, PACK * lo : PACK * hi])
 
-        blocks = [(0, 256), (256, 512), (512, 1024)]
-
-        def block_of(lo):
-            return min(lo // WIDE, 2)
-
-        def unit(t, lo, hi, on_vector=False):
-            r = block_of(lo)
-            acc = psum.tile([P, BANK], F32, name=f"acc2_{lo}_{t}", tag=f"bank{len(products) % BANKS}")
-            products.append(acc)
-            for n0 in range(lo, hi, WIDE):
-                n1 = min(hi, n0 + WIDE)
+        def decode(t, lo, hi, on_vector=False):
+            acc = psum.tile([P, BANK], F32, name=f"acc2_{lo}_{t}", tag=f"bank{len(banks_used) % BANKS}")
+            banks_used.append(acc)
+            cuts = [lo] + [c for c in z_cuts if lo < c < hi] + [hi]
+            for n0, n1 in zip(cuts, cuts[1:]):
                 nc.tensor.matmul_mx(
                     out=acc[:, n0 - lo : n1 - lo],
                     lhsT=w2_deal[:, 2 * P * t : 2 * P * (t + 1)].bitcast(FP4X4),
@@ -206,65 +203,63 @@ def tile_picked_sae8_relu_po_kernel(
                     start=True,
                     stop=True,
                 )
-            cols = slice(lo - r * WIDE, hi - r * WIDE)
+            plane = res[lo // MID][:, t, lo % MID : lo % MID + hi - lo]
             if on_vector:
-                nc.vector.tensor_scalar(res[r][:, t, cols], acc[:, 0 : hi - lo], b2_sb[:, t : t + 1], None, op0=ALU.add)
+                nc.vector.tensor_scalar(plane, acc[:, 0 : hi - lo], b2_sb[:, t : t + 1], None, op0=ALU.add)
             else:
-                nc.scalar.activation(res[r][:, t, cols], acc[:, 0 : hi - lo], ACT.Identity, bias=b2_sb[:, t : t + 1])
+                nc.scalar.activation(plane, acc[:, 0 : hi - lo], ACT.Identity, bias=b2_sb[:, t : t + 1])
 
-        def store(r, t0, t1, queue=nc.sync):
-            queue.dma_start(out_rows[:, t0:t1, blocks[r][0] : blocks[r][1]], res[r][:, t0:t1, :])
+        def store(t0, t1, lo, hi):
+            nc.sync.dma_start(out_rows[:, t0:t1, lo:hi], res_cols(t0, t1, lo, hi))
 
-        def round_result(lo, hi, engine_copy=nc.vector.tensor_copy):
-            r = block_of(lo)
-            engine_copy(
+        def round_result(lo, hi, copy=nc.vector.tensor_copy):
+            copy(
                 res_bf[:, lo:hi, :].rearrange("p (g i) t -> p g t i", i=4),
-                res[r][:, :, lo - r * WIDE : hi - r * WIDE].rearrange("p t (g i) -> p g t i", i=4),
+                res_cols(0, PACK, lo, hi).rearrange("p t (g i) -> p g t i", i=4),
             )
 
         def quantise_result(lo, hi):
             nc.vector.quantize_mx(out_words[:, lo:hi].bitcast(FP8X4), out_scales[:, lo:hi], res_bf[:, lo:hi, :].rearrange("p n t -> p (n t)"))
 
-        def store_words(lo, hi, queue=nc.sync):
-            queue.dma_start(out_1_rows[:, lo:hi], out_words[:, lo:hi].bitcast(I32))
+        lay_last_plane(0, EIGHTH)
+        lay_last_plane(EIGHTH, QUARTER)
+        quantise_z(0, EIGHTH)
+        quantise_z(EIGHTH, QUARTER)
+        lay_last_plane(SPLIT, U - QUARTER)
+        quantise_z(QUARTER, MID)
+        lay_last_plane(U - QUARTER, U)
+        quantise_z(MID, U - QUARTER)
+        quantise_z(U - QUARTER, U)
 
-        for r, (lo, hi) in enumerate(blocks):
-            res[r] = sb.tile([P, PACK, hi - lo], F32, name=f"res{r}", align_bytes=64)
-        lay(0, 128)
-        lay(128, 256)
-        quantise_z(0, 128)
-        quantise_z(128, 256)
-        lay(SPLIT, 768)
-        quantise_z(256, 512)
-        lay(768, U)
-        quantise_z(512, 768)
-        quantise_z(768, 1024)
-        for t in range(PACK):
-            unit(t, 0, 128)
-            unit(t, 128, 256)
-            store(0, t, t + 1)
-        for t in range(PACK):
-            unit(t, 256, 512, on_vector=t % 2 == 1)
-            if t % 2:
-                store(1, t - 1, t + 1)
+        decode(0, 0, EIGHTH)
+        decode(0, EIGHTH, QUARTER)
+        store(0, 1, 0, QUARTER)
+        decode(1, 0, QUARTER)
+        store(1, 2, 0, QUARTER)
+        for t in (2, 3):
+            decode(t, 0, MID)
+            store(t, t + 1, 0, MID)
         for t in (0, 1):
-            unit(t, 512, 1024)
-            store(2, t, t + 1)
-        for lo, hi in ((512, 768), (768, 896), (896, 1024)):
-            for t in (2, 3):
-                unit(t, lo, hi)
-        store(2, 2, PACK)
-        round_result(0, 256)
-        round_result(256, 512)
-        round_result(512, 768)
-        quantise_result(0, 512)
-        store_words(0, 512)
-        round_result(768, 896)
-        round_result(896, 1024, nc.scalar.copy)
-        quantise_result(512, 768)
-        quantise_result(768, 896)
-        quantise_result(896, 1024)
-        store_words(512, 1024, nc.scalar)
+            decode(t, QUARTER, MID, on_vector=True)
+        store(0, 2, QUARTER, MID)
+        last_pieces = [(MID, U - QUARTER), (U - QUARTER, U - EIGHTH), (U - EIGHTH, U)]
+        for t in range(PACK - 1):
+            decode(t, MID, U)
+            store(t, t + 1, MID, U)
+        for lo, hi in last_pieces:
+            decode(PACK - 1, lo, hi)
+        store(PACK - 1, PACK, MID, U)
+
+        round_result(0, QUARTER)
+        round_result(QUARTER, MID)
+        round_result(*last_pieces[0])
+        quantise_result(0, MID)
+        nc.sync.dma_start(out_1_rows[:, 0:MID], out_words[:, 0:MID].bitcast(I32))
+        round_result(*last_pieces[1])
+        round_result(*last_pieces[2], copy=nc.scalar.copy)
+        quantise_result(MID, U - QUARTER)
+        quantise_result(U - QUARTER, U)
+        nc.scalar.dma_start(out_1_rows[:, MID:U], out_words[:, MID:U].bitcast(I32))
         for q in range(4):
             queue = nc.sync if q % 2 == 0 else nc.scalar
             queue.dma_start(out_2[0, 4 * q : 4 * q + 4, :].bitcast(I32), out_scales[quadrant_rows(q), :].bitcast(I32))

@@ -28,7 +28,7 @@ FIRST = 128
 QUARTER = U // 4
 EIGHTH = U // 8
 MID = U // 2
-SPLIT = 640
+SPLIT = 576
 BACK = 704
 WARM_PASSES = 3
 
@@ -176,12 +176,9 @@ def tile_picked_sae8_relu_po_kernel(
         z_codes = sb.tile([P, U], U32, name="z_codes", align_bytes=64)
         z_scales = sb.tile([P, U], U8, name="z_scales", align_bytes=64)
         res_bf = sb.tile([P, U, PACK], BF16, name="res_bf", align_bytes=64)
-        res = [sb.tile([P, PACK, MID], F32, name=f"res{r}", align_bytes=64) for r in range(U // MID)]
+        res = sb.tile([P, PACK, U], F32, name="res", align_bytes=64)
         z_cuts = [0, EIGHTH, QUARTER, MID, U - QUARTER, U]
         banks_used = []
-
-        def res_cols(t0, t1, lo, hi):
-            return res[lo // MID][:, t0:t1, lo % MID : lo % MID + hi - lo]
 
         def lay_last_plane(lo, hi):
             nc.vector.tensor_copy(z_slots[:, lo:hi, PACK - 1], z[PACK - 1][:, lo:hi])
@@ -203,19 +200,18 @@ def tile_picked_sae8_relu_po_kernel(
                     start=True,
                     stop=True,
                 )
-            plane = res[lo // MID][:, t, lo % MID : lo % MID + hi - lo]
             if on_vector:
-                nc.vector.tensor_scalar(plane, acc[:, 0 : hi - lo], b2_sb[:, t : t + 1], None, op0=ALU.add)
+                nc.vector.tensor_scalar(res[:, t, lo:hi], acc[:, 0 : hi - lo], b2_sb[:, t : t + 1], None, op0=ALU.add)
             else:
-                nc.scalar.activation(plane, acc[:, 0 : hi - lo], ACT.Identity, bias=b2_sb[:, t : t + 1])
+                nc.scalar.activation(res[:, t, lo:hi], acc[:, 0 : hi - lo], ACT.Identity, bias=b2_sb[:, t : t + 1])
 
-        def store(t0, t1, lo, hi):
-            nc.sync.dma_start(out_rows[:, t0:t1, lo:hi], res_cols(t0, t1, lo, hi))
+        def store(t, lo, hi):
+            nc.sync.dma_start(out_rows[:, t : t + 1, lo:hi], res[:, t : t + 1, lo:hi])
 
         def round_result(lo, hi, copy=nc.vector.tensor_copy):
             copy(
                 res_bf[:, lo:hi, :].rearrange("p (g i) t -> p g t i", i=4),
-                res_cols(0, PACK, lo, hi).rearrange("p t (g i) -> p g t i", i=4),
+                res[:, :, lo:hi].rearrange("p t (g i) -> p g t i", i=4),
             )
 
         def quantise_result(lo, hi):
@@ -233,25 +229,28 @@ def tile_picked_sae8_relu_po_kernel(
 
         decode(0, 0, EIGHTH)
         decode(0, EIGHTH, QUARTER)
-        store(0, 1, 0, QUARTER)
+        store(0, 0, QUARTER)
         decode(1, 0, QUARTER)
-        store(1, 2, 0, QUARTER)
+        store(1, 0, QUARTER)
         for t in (2, 3):
             decode(t, 0, MID)
-            store(t, t + 1, 0, MID)
+            store(t, 0, MID)
         for t in (0, 1):
             decode(t, QUARTER, MID, on_vector=True)
-        store(0, 2, QUARTER, MID)
         last_pieces = [(MID, U - QUARTER), (U - QUARTER, U - EIGHTH), (U - EIGHTH, U)]
-        for t in range(PACK - 1):
-            decode(t, MID, U)
-            store(t, t + 1, MID, U)
+        decode(0, MID, U - QUARTER)
+        decode(0, U - QUARTER, U)
+        store(0, QUARTER, U)
+        decode(1, MID, U)
+        store(1, QUARTER, U)
+        decode(2, MID, U)
+        store(2, MID, U)
         for lo, hi in last_pieces:
-            decode(PACK - 1, lo, hi)
-        store(PACK - 1, PACK, MID, U)
+            decode(3, lo, hi)
+        store(3, MID, U)
 
-        round_result(0, QUARTER)
-        round_result(QUARTER, MID)
+        for lo in (0, QUARTER):
+            nc.vector.tensor_copy(res_bf[:, lo : lo + QUARTER, :], res[:, :, lo : lo + QUARTER].rearrange("p t n -> p n t"))
         round_result(*last_pieces[0])
         quantise_result(0, MID)
         nc.sync.dma_start(out_1_rows[:, 0:MID], out_words[:, 0:MID].bitcast(I32))

@@ -29,7 +29,7 @@ QUARTER = U // 4
 EIGHTH = U // 8
 MID = U // 2
 SPLIT = 576
-BACK = 704
+BACK = 640
 WARM_PASSES = 3
 
 
@@ -58,11 +58,11 @@ def tile_picked_sae8_relu_po_kernel(
 
         landing = P - SCALE_ROWS
         nc.sync.dma_start(offs_sb[:], offs)
-        nc.sync.dma_start(xs_tab[landing:P, :].bitcast(I32), x_scales[0].bitcast(I32))
+        nc.scalar.dma_start(xs_tab[landing:P, :].bitcast(I32), x_scales[0].bitcast(I32))
         nc.sync.dma_start(w1_raw[:], w1.rearrange("(p j) c -> p j c", j=PACK))
         nc.sync.dma_start(x_tab[:].bitcast(I32), x_words[0].rearrange("p c r -> p (c r)").bitcast(I32))
-        nc.sync.dma_start(held_sb[:], held)
         nc.sync.dma_start(b1_sb[:], b1.rearrange("(p t) o -> p (t o)", t=PACK))
+        nc.sync.dma_start(held_sb[:], held)
 
         warm = sb.tile([P, 8], F32, name="warm")
         nc.vector.memset(z[0][:], 0.0)
@@ -79,7 +79,8 @@ def tile_picked_sae8_relu_po_kernel(
         w1_codes, w1_scales = [], []
         for h in range(2):
             grouped = sb.tile([P, 2, P, PACK], BF16, name=f"w1_bf{h}", tag=f"stage{h}", align_bytes=64)
-            nc.scalar.copy(grouped[:].rearrange("p t m j -> p m j t"), w1_src[:, :, :, 2 * h : 2 * h + 2])
+            regroup = nc.vector.tensor_copy if h == 0 else nc.scalar.copy
+            regroup(grouped[:].rearrange("p t m j -> p m j t"), w1_src[:, :, :, 2 * h : 2 * h + 2])
             codes = sb.tile([P, 2 * P], U32, name=f"w1_codes{h}", align_bytes=64)
             scales = sb.tile([P, 2 * P], U8, name=f"w1_scales{h}", align_bytes=64)
             nc.vector.quantize_mx(codes[:].bitcast(FP8X4), scales[:], grouped[:].rearrange("p t m j -> p (t m j)"))
@@ -87,11 +88,8 @@ def tile_picked_sae8_relu_po_kernel(
             w1_scales.append(scales)
 
         x_pick = sb.tile([P, S], U32, name="x_pick", align_bytes=64)
-        for h in range(2):
-            nc.vector.tensor_copy(
-                x_pick[:, h * HALF : (h + 1) * HALF],
-                x_tab[:].indirect(offs_sb[:, h * HALF // GROUP : (h + 1) * HALF // GROUP]),
-            )
+        for lo, hi in ((0, FIRST), (FIRST, S)):
+            nc.vector.tensor_copy(x_pick[:, lo:hi], x_tab[:].indirect(offs_sb[:, lo // GROUP : hi // GROUP]))
 
         w2_raw = sb.tile([P, 2 * N], U8, name="w2_raw", tag="raw", align_bytes=64)
         w2s_raw = sb.tile([P, N], U8, name="w2s_raw", tag="stage0", align_bytes=64)
@@ -115,11 +113,11 @@ def tile_picked_sae8_relu_po_kernel(
         nc.sync.dma_start(b2_sb[:], b2.rearrange("(p t) o -> p (t o)", t=PACK))
 
         y = [sb.tile([P, S], F32, name=f"y{t}", tag=f"y{t}", align_bytes=64) for t in range(PACK)]
-        pieces = [(0, 0, FIRST), (1, 0, HALF), (0, FIRST, S), (1, HALF, S), (2, 0, S), (3, 0, S)]
+        pieces = [(0, 0, FIRST), (1, 0, FIRST), (0, FIRST, S), (1, FIRST, S), (2, 0, S), (3, 0, S)]
         for i, (t, lo, hi) in enumerate(pieces):
             acc = psum.tile([P, BANK], F32, name=f"acc1_{i}", tag=f"bank{i}")
             w1_cols = slice((t % 2) * P, (t % 2 + 1) * P)
-            cuts = [lo, HALF, hi] if lo < HALF < hi else [lo, hi]
+            cuts = [lo, HALF, hi] if lo == FIRST else [lo, hi]
             for n0, n1 in zip(cuts, cuts[1:]):
                 nc.tensor.matmul_mx(
                     out=acc[:, n0 - lo : n1 - lo],

@@ -29,8 +29,7 @@ QUARTER = U // 4
 EIGHTH = U // 8
 MID = U // 2
 SPLIT = 576
-BACK = 640
-WARM_PASSES = 3
+BACK = 768
 
 
 def tile_picked_sae8_relu_po_kernel(
@@ -49,38 +48,35 @@ def tile_picked_sae8_relu_po_kernel(
         offs_sb = lists.tile([P, S // GROUP], U16, name="offs_sb")
         held_sb = lists.tile([P, S // GROUP], U16, name="held_sb")
         w1_raw = sb.tile([P, PACK, H], F32, name="w1_raw", tag="raw", align_bytes=64)
-        x_tab = sb.tile([P, T], U32, name="x_tab", align_bytes=64)
+        x_tab = sb.tile([P, T], U32, name="x_tab", tag="table", align_bytes=64)
         xs_tab = sb.tile([P, T], U8, name="xs_tab", align_bytes=64)
         b1_sb = sb.tile([P, PACK], F32, name="b1_sb")
-        z = [sb.tile([P, U], F32, name=f"z{t}", align_bytes=64) for t in range(2)]
+        z = [sb.tile([P, U], F32, name=f"z{t}", tag=f"z{t}", align_bytes=64) for t in range(2)]
         xs_pick = sb.tile([P, S], U8, name="xs_pick", align_bytes=64)
         xs_rows = sb.tile([P, S], U8, name="xs_rows", align_bytes=64)
 
         landing = P - SCALE_ROWS
         nc.sync.dma_start(offs_sb[:], offs)
         nc.scalar.dma_start(xs_tab[landing:P, :].bitcast(I32), x_scales[0].bitcast(I32))
+        nc.scalar.dma_start(b1_sb[:], b1.rearrange("(p t) o -> p (t o)", t=PACK))
         nc.sync.dma_start(w1_raw[:], w1.rearrange("(p j) c -> p j c", j=PACK))
         nc.sync.dma_start(x_tab[:].bitcast(I32), x_words[0].rearrange("p c r -> p (c r)").bitcast(I32))
-        nc.sync.dma_start(b1_sb[:], b1.rearrange("(p t) o -> p (t o)", t=PACK))
         nc.sync.dma_start(held_sb[:], held)
-
-        warm = sb.tile([P, 8], F32, name="warm")
-        nc.vector.memset(z[0][:], 0.0)
-        nc.scalar.activation(warm[:], z[0][:, 0:8], ACT.Relu)
 
         nc.vector.memset(xs_tab[0:landing, :].bitcast(I32), 0)
         nc.vector.memset(xs_pick[:].bitcast(I32), 0)
         nc.vector.tensor_copy(xs_rows[:], xs_tab[:].indirect(offs_sb[:]))
         for q in range(4):
             nc.scalar.dma_start(xs_pick[quadrant_rows(q), :].bitcast(I32), xs_rows[landing + 4 * q : landing + 4 * q + 4, :].bitcast(I32))
-        nc.vector.memset(z[1][:], 0.0)
+        for t in range(2):
+            nc.vector.memset(z[t][:], 0.0)
 
         w1_src = w1_raw[:].rearrange("p j (m t) -> p m j t", t=PACK)
-        w1_codes, w1_scales = [], []
+        w1_bf, w1_codes, w1_scales = [], [], []
         for h in range(2):
-            grouped = sb.tile([P, 2, P, PACK], BF16, name=f"w1_bf{h}", tag=f"stage{h}", align_bytes=64)
-            regroup = nc.vector.tensor_copy if h == 0 else nc.scalar.copy
-            regroup(grouped[:].rearrange("p t m j -> p m j t"), w1_src[:, :, :, 2 * h : 2 * h + 2])
+            w1_bf.append(sb.tile([P, 2, P, PACK], BF16, name=f"w1_bf{h}", tag=f"stage{h}", align_bytes=64))
+            nc.vector.tensor_copy(w1_bf[h][:].rearrange("p t m j -> p m j t"), w1_src[:, :, :, 2 * h : 2 * h + 2])
+        for h, grouped in enumerate(w1_bf):
             codes = sb.tile([P, 2 * P], U32, name=f"w1_codes{h}", align_bytes=64)
             scales = sb.tile([P, 2 * P], U8, name=f"w1_scales{h}", align_bytes=64)
             nc.vector.quantize_mx(codes[:].bitcast(FP8X4), scales[:], grouped[:].rearrange("p t m j -> p (t m j)"))
@@ -92,9 +88,9 @@ def tile_picked_sae8_relu_po_kernel(
             nc.vector.tensor_copy(x_pick[:, lo:hi], x_tab[:].indirect(offs_sb[:, lo // GROUP : hi // GROUP]))
 
         w2_raw = sb.tile([P, 2 * N], U8, name="w2_raw", tag="raw", align_bytes=64)
-        w2s_raw = sb.tile([P, N], U8, name="w2s_raw", tag="stage0", align_bytes=64)
+        w2s_raw = sb.tile([P, N], U8, name="w2s_raw", tag="stage1", align_bytes=64)
         w2_deal = sb.tile([P, 2 * N], U8, name="w2_deal", align_bytes=64)
-        z.append(sb.tile([P, U], F32, name="z2", tag="stage1", align_bytes=64))
+        z.append(sb.tile([P, U], F32, name="z2", tag="table", align_bytes=64))
         nc.gpsimd.memset(z[2][:], 0.0)
         w2s_deal = sb.tile([P, N], U8, name="w2s_deal", align_bytes=64)
         nc.sync.dma_start(w2_raw[:].bitcast(I32), w2_words[0].bitcast(I32))
@@ -102,15 +98,9 @@ def tile_picked_sae8_relu_po_kernel(
         for q in range(4):
             nc.sync.dma_start(w2s_raw[quadrant_rows(q), :].bitcast(I32), w2_scales[0, 4 * q : 4 * q + 4, :].bitcast(I32))
         nc.gpsimd.tensor_copy(
-            w2_deal[:].rearrange("p (t m b) -> p t m b", t=PACK, b=2),
-            w2_raw[:].rearrange("p (m t b) -> p t m b", t=PACK, b=2),
-        )
-        nc.gpsimd.tensor_copy(
             w2s_deal[:].rearrange("p (t m) -> p t m", t=PACK),
             w2s_raw[:].rearrange("p (m t) -> p t m", t=PACK),
         )
-        b2_sb = sb.tile([P, PACK], F32, name="b2_sb", tag="raw", align_bytes=64)
-        nc.sync.dma_start(b2_sb[:], b2.rearrange("(p t) o -> p (t o)", t=PACK))
 
         y = [sb.tile([P, S], F32, name=f"y{t}", tag=f"y{t}", align_bytes=64) for t in range(PACK)]
         pieces = [(0, 0, FIRST), (1, 0, FIRST), (0, FIRST, S), (1, FIRST, S), (2, 0, S), (3, 0, S)]
@@ -130,6 +120,11 @@ def tile_picked_sae8_relu_po_kernel(
                 )
             nc.scalar.activation(y[t][:, lo:hi], acc[:, 0 : hi - lo], ACT.Relu, bias=b1_sb[:, t : t + 1])
 
+        nc.scalar.copy(
+            w2_deal[:].bitcast(U16).rearrange("p (t m) -> p t m", t=PACK),
+            w2_raw[:].bitcast(U16).rearrange("p (m t) -> p t m", t=PACK),
+        )
+
         z_bf = sb.tile([P, U * PACK], BF16, name="z_bf", align_bytes=64)
         z_slots = z_bf[:].rearrange("p (w t) -> p w t", t=PACK)
 
@@ -144,24 +139,14 @@ def tile_picked_sae8_relu_po_kernel(
             if hi == S and t < 2:
                 nc.scalar.copy(z_slots[:, 0:BACK, t], z[t][:, 0:BACK])
                 nc.gpsimd.tensor_scalar(z_slots[:, BACK:U, t], z[t][:, BACK:U], 1.0, 0.0, op0=ALU.mult, op1=ALU.add)
+            if hi == S and t == 1:
+                b2_sb = sb.tile([P, PACK], F32, name="b2_sb", tag="z1", align_bytes=64)
+                nc.sync.dma_start(b2_sb[:], b2.rearrange("(p t) o -> p (t o)", t=PACK))
             if t == 2:
                 nc.scalar.copy(z_slots[:, 0:QUARTER, t:PACK], both_slots(t, 0, QUARTER))
                 nc.scalar.copy(z_slots[:, QUARTER:SPLIT, t], z[t][:, QUARTER:SPLIT])
                 nc.scalar.copy(z_slots[:, SPLIT:BACK, t:PACK], both_slots(t, SPLIT, BACK))
                 nc.gpsimd.tensor_scalar(z_slots[:, BACK:U, t:PACK], both_slots(t, BACK, U), 1.0, 0.0, op0=ALU.mult, op1=ALU.add)
-                w2s_late = sb.tile([P, N], U8, name="w2s_late", tag="y2", align_bytes=64)
-                nc.gpsimd.tensor_copy(w2s_late[:].bitcast(I32), w2s_deal[:].bitcast(I32))
-                unread = psum.tile([P, BANK], F32, name="unread", tag=f"bank{BANKS - 1}")
-                for rep in range(WARM_PASSES):
-                    nc.tensor.matmul_mx(
-                        out=unread[:],
-                        lhsT=w2_deal[:, 0 : 2 * P].bitcast(FP4X4),
-                        lhsT_scale=w2s_late[:, 0:P],
-                        rhs=x_pick[:].bitcast(FP8X4),
-                        rhs_scale=xs_pick[:],
-                        start=True,
-                        stop=True,
-                    )
 
         for lo, hi in ((QUARTER, MID), (MID, SPLIT)):
             nc.scalar.copy(z_slots[:, lo:hi, PACK - 1], z[PACK - 1][:, lo:hi])
@@ -192,7 +177,7 @@ def tile_picked_sae8_relu_po_kernel(
                 nc.tensor.matmul_mx(
                     out=acc[:, n0 - lo : n1 - lo],
                     lhsT=w2_deal[:, 2 * P * t : 2 * P * (t + 1)].bitcast(FP4X4),
-                    lhsT_scale=w2s_late[:, P * t : P * (t + 1)],
+                    lhsT_scale=w2s_deal[:, P * t : P * (t + 1)],
                     rhs=z_codes[:, n0:n1].bitcast(FP8X4),
                     rhs_scale=z_scales[:, n0:n1],
                     start=True,

@@ -29,7 +29,7 @@ QUARTER = U // 4
 EIGHTH = U // 8
 MID = U // 2
 SPLIT = 576
-BACK = 768
+BACK = 704
 
 
 def tile_picked_sae8_relu_po_kernel(
@@ -49,8 +49,7 @@ def tile_picked_sae8_relu_po_kernel(
         held_sb = lists.tile([P, S // GROUP], U16, name="held_sb")
         w1_raw = sb.tile([P, PACK, H], F32, name="w1_raw", tag="raw", align_bytes=64)
         x_tab = sb.tile([P, T], U32, name="x_tab", tag="table", align_bytes=64)
-        xs_tab = sb.tile([P, T], U8, name="xs_tab", align_bytes=64)
-        b1_sb = sb.tile([P, PACK], F32, name="b1_sb")
+        xs_tab = sb.tile([P, T], U8, name="xs_tab", tag="rows", align_bytes=64)
         z = [sb.tile([P, U], F32, name=f"z{t}", tag=f"z{t}", align_bytes=64) for t in range(2)]
         xs_pick = sb.tile([P, S], U8, name="xs_pick", align_bytes=64)
         xs_rows = sb.tile([P, S], U8, name="xs_rows", align_bytes=64)
@@ -58,7 +57,6 @@ def tile_picked_sae8_relu_po_kernel(
         landing = P - SCALE_ROWS
         nc.sync.dma_start(offs_sb[:], offs)
         nc.scalar.dma_start(xs_tab[landing:P, :].bitcast(I32), x_scales[0].bitcast(I32))
-        nc.scalar.dma_start(b1_sb[:], b1.rearrange("(p t) o -> p (t o)", t=PACK))
         nc.sync.dma_start(w1_raw[:], w1.rearrange("(p j) c -> p j c", j=PACK))
         nc.sync.dma_start(x_tab[:].bitcast(I32), x_words[0].rearrange("p c r -> p (c r)").bitcast(I32))
         nc.sync.dma_start(held_sb[:], held)
@@ -67,21 +65,23 @@ def tile_picked_sae8_relu_po_kernel(
         nc.vector.memset(xs_pick[:].bitcast(I32), 0)
         nc.vector.tensor_copy(xs_rows[:], xs_tab[:].indirect(offs_sb[:]))
         for q in range(4):
-            nc.scalar.dma_start(xs_pick[quadrant_rows(q), :].bitcast(I32), xs_rows[landing + 4 * q : landing + 4 * q + 4, :].bitcast(I32))
+            nc.sync.dma_start(xs_pick[quadrant_rows(q), :].bitcast(I32), xs_rows[landing + 4 * q : landing + 4 * q + 4, :].bitcast(I32))
+        b1_sb = sb.tile([P, PACK], F32, name="b1_sb", tag="rows", align_bytes=64)
+        nc.sync.dma_start(b1_sb[:], b1.rearrange("(p t) o -> p (t o)", t=PACK))
         for t in range(2):
             nc.vector.memset(z[t][:], 0.0)
 
         w1_src = w1_raw[:].rearrange("p j (m t) -> p m j t", t=PACK)
-        w1_bf, w1_codes, w1_scales = [], [], []
+        w1_bf = []
+        w1_codes = sb.tile([P, H], U32, name="w1_codes", align_bytes=64)
+        w1_scales = sb.tile([P, H], U8, name="w1_scales", align_bytes=64)
         for h in range(2):
             w1_bf.append(sb.tile([P, 2, P, PACK], BF16, name=f"w1_bf{h}", tag=f"stage{h}", align_bytes=64))
-            nc.vector.tensor_copy(w1_bf[h][:].rearrange("p t m j -> p m j t"), w1_src[:, :, :, 2 * h : 2 * h + 2])
+        nc.vector.tensor_copy(w1_bf[0][:].rearrange("p t m j -> p m j t"), w1_src[:, :, :, 0:2])
+        nc.scalar.copy(w1_bf[1][:].rearrange("p t m j -> p m j t"), w1_src[:, :, :, 2:4])
         for h, grouped in enumerate(w1_bf):
-            codes = sb.tile([P, 2 * P], U32, name=f"w1_codes{h}", align_bytes=64)
-            scales = sb.tile([P, 2 * P], U8, name=f"w1_scales{h}", align_bytes=64)
-            nc.vector.quantize_mx(codes[:].bitcast(FP8X4), scales[:], grouped[:].rearrange("p t m j -> p (t m j)"))
-            w1_codes.append(codes)
-            w1_scales.append(scales)
+            cols = slice(2 * P * h, 2 * P * (h + 1))
+            nc.vector.quantize_mx(w1_codes[:, cols].bitcast(FP8X4), w1_scales[:, cols], grouped[:].rearrange("p t m j -> p (t m j)"))
 
         x_pick = sb.tile([P, S], U32, name="x_pick", align_bytes=64)
         for lo, hi in ((0, FIRST), (FIRST, S)):
@@ -89,7 +89,6 @@ def tile_picked_sae8_relu_po_kernel(
 
         w2_raw = sb.tile([P, 2 * N], U8, name="w2_raw", tag="raw", align_bytes=64)
         w2s_raw = sb.tile([P, N], U8, name="w2s_raw", tag="stage1", align_bytes=64)
-        w2_deal = sb.tile([P, 2 * N], U8, name="w2_deal", align_bytes=64)
         z.append(sb.tile([P, U], F32, name="z2", tag="table", align_bytes=64))
         nc.gpsimd.memset(z[2][:], 0.0)
         w2s_deal = sb.tile([P, N], U8, name="w2s_deal", align_bytes=64)
@@ -106,24 +105,19 @@ def tile_picked_sae8_relu_po_kernel(
         pieces = [(0, 0, FIRST), (1, 0, FIRST), (0, FIRST, S), (1, FIRST, S), (2, 0, S), (3, 0, S)]
         for i, (t, lo, hi) in enumerate(pieces):
             acc = psum.tile([P, BANK], F32, name=f"acc1_{i}", tag=f"bank{i}")
-            w1_cols = slice((t % 2) * P, (t % 2 + 1) * P)
+            w1_cols = slice(t * P, (t + 1) * P)
             cuts = [lo, HALF, hi] if lo == FIRST else [lo, hi]
             for n0, n1 in zip(cuts, cuts[1:]):
                 nc.tensor.matmul_mx(
                     out=acc[:, n0 - lo : n1 - lo],
-                    lhsT=w1_codes[t // 2][:, w1_cols].bitcast(FP8X4),
-                    lhsT_scale=w1_scales[t // 2][:, w1_cols],
+                    lhsT=w1_codes[:, w1_cols].bitcast(FP8X4),
+                    lhsT_scale=w1_scales[:, w1_cols],
                     rhs=x_pick[:, n0:n1].bitcast(FP8X4),
                     rhs_scale=xs_pick[:, n0:n1],
                     start=True,
                     stop=True,
                 )
             nc.scalar.activation(y[t][:, lo:hi], acc[:, 0 : hi - lo], ACT.Relu, bias=b1_sb[:, t : t + 1])
-
-        nc.scalar.copy(
-            w2_deal[:].bitcast(U16).rearrange("p (t m) -> p t m", t=PACK),
-            w2_raw[:].bitcast(U16).rearrange("p (m t) -> p t m", t=PACK),
-        )
 
         z_bf = sb.tile([P, U * PACK], BF16, name="z_bf", align_bytes=64)
         z_slots = z_bf[:].rearrange("p (w t) -> p w t", t=PACK)
@@ -147,6 +141,11 @@ def tile_picked_sae8_relu_po_kernel(
                 nc.scalar.copy(z_slots[:, QUARTER:SPLIT, t], z[t][:, QUARTER:SPLIT])
                 nc.scalar.copy(z_slots[:, SPLIT:BACK, t:PACK], both_slots(t, SPLIT, BACK))
                 nc.gpsimd.tensor_scalar(z_slots[:, BACK:U, t:PACK], both_slots(t, BACK, U), 1.0, 0.0, op0=ALU.mult, op1=ALU.add)
+                w2_deal = sb.tile([P, 2 * N], U8, name="w2_deal", tag="y2", align_bytes=64)
+                nc.scalar.copy(
+                    w2_deal[:].bitcast(U16).rearrange("p (t m) -> p t m", t=PACK),
+                    w2_raw[:].bitcast(U16).rearrange("p (m t) -> p t m", t=PACK),
+                )
 
         for lo, hi in ((QUARTER, MID), (MID, SPLIT)):
             nc.scalar.copy(z_slots[:, lo:hi, PACK - 1], z[PACK - 1][:, lo:hi])
@@ -160,7 +159,6 @@ def tile_picked_sae8_relu_po_kernel(
         z_scales = sb.tile([P, U], U8, name="z_scales", align_bytes=64)
         res_bf = sb.tile([P, U, PACK], BF16, name="res_bf", align_bytes=64)
         res = sb.tile([P, PACK, U], F32, name="res", align_bytes=64)
-        z_cuts = [0, EIGHTH, QUARTER, MID, U - QUARTER, U]
         banks_used = []
 
         def lay_last_plane(lo, hi):
@@ -172,17 +170,15 @@ def tile_picked_sae8_relu_po_kernel(
         def decode(t, lo, hi, on_vector=False):
             acc = psum.tile([P, BANK], F32, name=f"acc2_{lo}_{t}", tag=f"bank{len(banks_used) % BANKS}")
             banks_used.append(acc)
-            cuts = [lo] + [c for c in z_cuts if lo < c < hi] + [hi]
-            for n0, n1 in zip(cuts, cuts[1:]):
-                nc.tensor.matmul_mx(
-                    out=acc[:, n0 - lo : n1 - lo],
-                    lhsT=w2_deal[:, 2 * P * t : 2 * P * (t + 1)].bitcast(FP4X4),
-                    lhsT_scale=w2s_deal[:, P * t : P * (t + 1)],
-                    rhs=z_codes[:, n0:n1].bitcast(FP8X4),
-                    rhs_scale=z_scales[:, n0:n1],
-                    start=True,
-                    stop=True,
-                )
+            nc.tensor.matmul_mx(
+                out=acc[:, 0 : hi - lo],
+                lhsT=w2_deal[:, 2 * P * t : 2 * P * (t + 1)].bitcast(FP4X4),
+                lhsT_scale=w2s_deal[:, P * t : P * (t + 1)],
+                rhs=z_codes[:, lo:hi].bitcast(FP8X4),
+                rhs_scale=z_scales[:, lo:hi],
+                start=True,
+                stop=True,
+            )
             if on_vector:
                 nc.vector.tensor_scalar(res[:, t, lo:hi], acc[:, 0 : hi - lo], b2_sb[:, t : t + 1], None, op0=ALU.add)
             else:
@@ -215,9 +211,11 @@ def tile_picked_sae8_relu_po_kernel(
         store(0, 0, QUARTER)
         decode(1, 0, QUARTER)
         store(1, 0, QUARTER)
-        for t in (2, 3):
-            decode(t, 0, MID)
-            store(t, 0, MID)
+        decode(2, 0, QUARTER)
+        decode(2, QUARTER, MID)
+        store(2, 0, MID)
+        decode(3, 0, MID)
+        store(3, 0, MID)
         for t in (0, 1):
             decode(t, QUARTER, MID, on_vector=True)
         last_pieces = [(MID, U - QUARTER), (U - QUARTER, U - EIGHTH), (U - EIGHTH, U)]

@@ -146,6 +146,16 @@ def tile_picked_sae8_relu_po_kernel(
                     w2_deal[:].bitcast(U16).rearrange("p (t m) -> p t m", t=PACK),
                     w2_raw[:].bitcast(U16).rearrange("p (m t) -> p t m", t=PACK),
                 )
+                unread = psum.tile([P, BANK], F32, name="unread", tag=f"bank{BANKS - 1}")
+                nc.tensor.matmul_mx(
+                    out=unread[:],
+                    lhsT=w2_deal[:, 0 : 2 * P].bitcast(FP4X4),
+                    lhsT_scale=w2s_deal[:, 0:P],
+                    rhs=w1_codes[:].bitcast(FP8X4),
+                    rhs_scale=w1_scales[:],
+                    start=True,
+                    stop=True,
+                )
 
         for lo, hi in ((QUARTER, MID), (MID, SPLIT)):
             nc.scalar.copy(z_slots[:, lo:hi, PACK - 1], z[PACK - 1][:, lo:hi])

@@ -137,10 +137,6 @@ def tile_picked_sae8_relu_po_kernel(
                 b2_sb = sb.tile([P, PACK], F32, name="b2_sb", tag="z1", align_bytes=64)
                 nc.sync.dma_start(b2_sb[:], b2.rearrange("(p t) o -> p (t o)", t=PACK))
             if t == 2:
-                nc.scalar.copy(z_slots[:, 0:QUARTER, t:PACK], both_slots(t, 0, QUARTER))
-                nc.scalar.copy(z_slots[:, QUARTER:SPLIT, t], z[t][:, QUARTER:SPLIT])
-                nc.scalar.copy(z_slots[:, SPLIT:BACK, t:PACK], both_slots(t, SPLIT, BACK))
-                nc.gpsimd.tensor_scalar(z_slots[:, BACK:U, t:PACK], both_slots(t, BACK, U), 1.0, 0.0, op0=ALU.mult, op1=ALU.add)
                 w2_deal = sb.tile([P, 2 * N], U8, name="w2_deal", tag="y2", align_bytes=64)
                 nc.scalar.copy(
                     w2_deal[:].bitcast(U16).rearrange("p (t m) -> p t m", t=PACK),
@@ -148,14 +144,28 @@ def tile_picked_sae8_relu_po_kernel(
                 )
                 unread = psum.tile([P, BANK], F32, name="unread", tag=f"bank{BANKS - 1}")
                 nc.tensor.matmul_mx(
-                    out=unread[:],
-                    lhsT=w2_deal[:, 0 : 2 * P].bitcast(FP4X4),
-                    lhsT_scale=w2s_deal[:, 0:P],
-                    rhs=w1_codes[:].bitcast(FP8X4),
-                    rhs_scale=w1_scales[:],
+                    out=unread[:, 0:64],
+                    lhsT=w1_codes[:, 0:P].bitcast(FP8X4),
+                    lhsT_scale=w1_scales[:, 0:P],
+                    rhs=w2_deal[:, 0:128].bitcast(FP4X4),
+                    rhs_scale=w2s_deal[:, 0:64],
                     start=True,
                     stop=True,
                 )
+                for rep in range(4):
+                    nc.tensor.matmul_mx(
+                        out=unread[0:32, :],
+                        lhsT=w1_codes[:, 0:32].bitcast(FP8X4),
+                        lhsT_scale=w1_scales[:, 0:32],
+                        rhs=w1_codes[:].bitcast(FP8X4),
+                        rhs_scale=w1_scales[:],
+                        start=True,
+                        stop=True,
+                    )
+                nc.scalar.copy(z_slots[:, 0:QUARTER, t:PACK], both_slots(t, 0, QUARTER))
+                nc.scalar.copy(z_slots[:, QUARTER:SPLIT, t], z[t][:, QUARTER:SPLIT])
+                nc.scalar.copy(z_slots[:, SPLIT:BACK, t:PACK], both_slots(t, SPLIT, BACK))
+                nc.gpsimd.tensor_scalar(z_slots[:, BACK:U, t:PACK], both_slots(t, BACK, U), 1.0, 0.0, op0=ALU.mult, op1=ALU.add)
 
         for lo, hi in ((QUARTER, MID), (MID, SPLIT)):
             nc.scalar.copy(z_slots[:, lo:hi, PACK - 1], z[PACK - 1][:, lo:hi])

@@ -23,13 +23,17 @@ QUADRANT = 32
 SCALE_ROWS = 16
 BANK = 512
 BANKS = 8
-HALF = S // 2
 FIRST = 128
-QUARTER = U // 4
+HALF = S // 2
 EIGHTH = U // 8
+QUARTER = U // 4
 MID = U // 2
-SPLIT = 576
-BACK = 704
+LAST = U - QUARTER
+FRONT = 320
+SPLIT = 640
+WARM_PASSES = 4
+WARM_ROWS = 32
+WARM_GATE = 64
 
 
 def tile_picked_sae8_relu_po_kernel(
@@ -39,6 +43,9 @@ def tile_picked_sae8_relu_po_kernel(
 
     def quadrant_rows(q):
         return slice(QUADRANT * q, QUADRANT * q + 4)
+
+    def mx_pass(out, lhsT, lhsT_scale, rhs, rhs_scale):
+        nc.tensor.matmul_mx(out=out, lhsT=lhsT, lhsT_scale=lhsT_scale, rhs=rhs, rhs_scale=rhs_scale, start=True, stop=True)
 
     with ExitStack() as ctx:
         lists = ctx.enter_context(tc.tile_pool(name="lists", bufs=1))
@@ -50,7 +57,7 @@ def tile_picked_sae8_relu_po_kernel(
         w1_raw = sb.tile([P, PACK, H], F32, name="w1_raw", tag="raw", align_bytes=64)
         x_tab = sb.tile([P, T], U32, name="x_tab", tag="table", align_bytes=64)
         xs_tab = sb.tile([P, T], U8, name="xs_tab", tag="rows", align_bytes=64)
-        z = [sb.tile([P, U], F32, name=f"z{t}", tag=f"z{t}", align_bytes=64) for t in range(2)]
+        z = [sb.tile([P, U], F32, name=f"z{t}", align_bytes=64) for t in range(2)]
         xs_pick = sb.tile([P, S], U8, name="xs_pick", align_bytes=64)
         xs_rows = sb.tile([P, S], U8, name="xs_rows", align_bytes=64)
 
@@ -72,16 +79,14 @@ def tile_picked_sae8_relu_po_kernel(
             nc.vector.memset(z[t][:], 0.0)
 
         w1_src = w1_raw[:].rearrange("p j (m t) -> p m j t", t=PACK)
-        w1_bf = []
         w1_codes = sb.tile([P, H], U32, name="w1_codes", align_bytes=64)
         w1_scales = sb.tile([P, H], U8, name="w1_scales", align_bytes=64)
+        w1_bf = [sb.tile([P, 2, P, PACK], BF16, name=f"w1_bf{h}", tag=f"stage{h}", align_bytes=64) for h in range(2)]
+        for h, copy in enumerate((nc.vector.tensor_copy, nc.scalar.copy)):
+            copy(w1_bf[h][:].rearrange("p t m j -> p m j t"), w1_src[:, :, :, 2 * h : 2 * h + 2])
         for h in range(2):
-            w1_bf.append(sb.tile([P, 2, P, PACK], BF16, name=f"w1_bf{h}", tag=f"stage{h}", align_bytes=64))
-        nc.vector.tensor_copy(w1_bf[0][:].rearrange("p t m j -> p m j t"), w1_src[:, :, :, 0:2])
-        nc.scalar.copy(w1_bf[1][:].rearrange("p t m j -> p m j t"), w1_src[:, :, :, 2:4])
-        for h, grouped in enumerate(w1_bf):
             cols = slice(2 * P * h, 2 * P * (h + 1))
-            nc.vector.quantize_mx(w1_codes[:, cols].bitcast(FP8X4), w1_scales[:, cols], grouped[:].rearrange("p t m j -> p (t m j)"))
+            nc.vector.quantize_mx(w1_codes[:, cols].bitcast(FP8X4), w1_scales[:, cols], w1_bf[h][:].rearrange("p t m j -> p (t m j)"))
 
         x_pick = sb.tile([P, S], U32, name="x_pick", align_bytes=64)
         for lo, hi in ((0, FIRST), (FIRST, S)):
@@ -108,16 +113,17 @@ def tile_picked_sae8_relu_po_kernel(
             w1_cols = slice(t * P, (t + 1) * P)
             cuts = [lo, HALF, hi] if lo == FIRST else [lo, hi]
             for n0, n1 in zip(cuts, cuts[1:]):
-                nc.tensor.matmul_mx(
-                    out=acc[:, n0 - lo : n1 - lo],
-                    lhsT=w1_codes[:, w1_cols].bitcast(FP8X4),
-                    lhsT_scale=w1_scales[:, w1_cols],
-                    rhs=x_pick[:, n0:n1].bitcast(FP8X4),
-                    rhs_scale=xs_pick[:, n0:n1],
-                    start=True,
-                    stop=True,
+                mx_pass(
+                    acc[:, n0 - lo : n1 - lo],
+                    w1_codes[:, w1_cols].bitcast(FP8X4),
+                    w1_scales[:, w1_cols],
+                    x_pick[:, n0:n1].bitcast(FP8X4),
+                    xs_pick[:, n0:n1],
                 )
             nc.scalar.activation(y[t][:, lo:hi], acc[:, 0 : hi - lo], ACT.Relu, bias=b1_sb[:, t : t + 1])
+
+        b2_sb = sb.tile([P, PACK], F32, name="b2_sb", tag="stage0", align_bytes=64)
+        nc.sync.dma_start(b2_sb[:], b2.rearrange("(p t) o -> p (t o)", t=PACK))
 
         z_bf = sb.tile([P, U * PACK], BF16, name="z_bf", align_bytes=64)
         z_slots = z_bf[:].rearrange("p (w t) -> p w t", t=PACK)
@@ -131,11 +137,8 @@ def tile_picked_sae8_relu_po_kernel(
                 z.append(sb.tile([P, U], F32, name="z3", tag="y0", align_bytes=64))
                 nc.gpsimd.memset(z[3][:], 0.0)
             if hi == S and t < 2:
-                nc.scalar.copy(z_slots[:, 0:BACK, t], z[t][:, 0:BACK])
-                nc.gpsimd.tensor_scalar(z_slots[:, BACK:U, t], z[t][:, BACK:U], 1.0, 0.0, op0=ALU.mult, op1=ALU.add)
-            if hi == S and t == 1:
-                b2_sb = sb.tile([P, PACK], F32, name="b2_sb", tag="z1", align_bytes=64)
-                nc.sync.dma_start(b2_sb[:], b2.rearrange("(p t) o -> p (t o)", t=PACK))
+                nc.scalar.copy(z_slots[:, 0:SPLIT, t], z[t][:, 0:SPLIT])
+                nc.gpsimd.tensor_scalar(z_slots[:, SPLIT:U, t], z[t][:, SPLIT:U], 1.0, 0.0, op0=ALU.mult, op1=ALU.add)
             if t == 2:
                 w2_deal = sb.tile([P, 2 * N], U8, name="w2_deal", tag="y2", align_bytes=64)
                 nc.scalar.copy(
@@ -143,31 +146,26 @@ def tile_picked_sae8_relu_po_kernel(
                     w2_raw[:].bitcast(U16).rearrange("p (m t) -> p t m", t=PACK),
                 )
                 unread = psum.tile([P, BANK], F32, name="unread", tag=f"bank{BANKS - 1}")
-                nc.tensor.matmul_mx(
-                    out=unread[:, 0:64],
-                    lhsT=w1_codes[:, 0:P].bitcast(FP8X4),
-                    lhsT_scale=w1_scales[:, 0:P],
-                    rhs=w2_deal[:, 0:128].bitcast(FP4X4),
-                    rhs_scale=w2s_deal[:, 0:64],
-                    start=True,
-                    stop=True,
+                mx_pass(
+                    unread[:, 0:WARM_GATE],
+                    w1_codes[:, 0:P].bitcast(FP8X4),
+                    w1_scales[:, 0:P],
+                    w2_deal[:, 0 : 2 * WARM_GATE].bitcast(FP4X4),
+                    w2s_deal[:, 0:WARM_GATE],
                 )
-                for rep in range(4):
-                    nc.tensor.matmul_mx(
-                        out=unread[0:32, :],
-                        lhsT=w1_codes[:, 0:32].bitcast(FP8X4),
-                        lhsT_scale=w1_scales[:, 0:32],
-                        rhs=w1_codes[:].bitcast(FP8X4),
-                        rhs_scale=w1_scales[:],
-                        start=True,
-                        stop=True,
+                for rep in range(WARM_PASSES):
+                    mx_pass(
+                        unread[0:WARM_ROWS, :],
+                        w1_codes[:, 0:WARM_ROWS].bitcast(FP8X4),
+                        w1_scales[:, 0:WARM_ROWS],
+                        w1_codes[:].bitcast(FP8X4),
+                        w1_scales[:],
                     )
-                nc.scalar.copy(z_slots[:, 0:QUARTER, t:PACK], both_slots(t, 0, QUARTER))
-                nc.scalar.copy(z_slots[:, QUARTER:SPLIT, t], z[t][:, QUARTER:SPLIT])
-                nc.scalar.copy(z_slots[:, SPLIT:BACK, t:PACK], both_slots(t, SPLIT, BACK))
-                nc.gpsimd.tensor_scalar(z_slots[:, BACK:U, t:PACK], both_slots(t, BACK, U), 1.0, 0.0, op0=ALU.mult, op1=ALU.add)
+                nc.scalar.copy(z_slots[:, 0:FRONT, t:PACK], both_slots(t, 0, FRONT))
+                nc.scalar.copy(z_slots[:, FRONT:SPLIT, t], z[t][:, FRONT:SPLIT])
+                nc.gpsimd.tensor_scalar(z_slots[:, SPLIT:U, t:PACK], both_slots(t, SPLIT, U), 1.0, 0.0, op0=ALU.mult, op1=ALU.add)
 
-        for lo, hi in ((QUARTER, MID), (MID, SPLIT)):
+        for lo, hi in ((FRONT, MID), (MID, SPLIT)):
             nc.scalar.copy(z_slots[:, lo:hi, PACK - 1], z[PACK - 1][:, lo:hi])
 
         out_words = sb.tile([P, U], U32, name="out_words", align_bytes=64)
@@ -178,8 +176,23 @@ def tile_picked_sae8_relu_po_kernel(
         z_codes = sb.tile([P, U], U32, name="z_codes", align_bytes=64)
         z_scales = sb.tile([P, U], U8, name="z_scales", align_bytes=64)
         res_bf = sb.tile([P, U, PACK], BF16, name="res_bf", align_bytes=64)
-        res = sb.tile([P, PACK, U], F32, name="res", align_bytes=64)
         banks_used = []
+
+        pitch = (PACK + 1) * MID
+        first_at = 2 * pitch + MID
+        res = sb.tile([P, PACK * pitch], F32, name="res", align_bytes=64)
+        halves = [
+            res[:, first_at : first_at + PACK * MID].rearrange("p (t w) -> p t w", t=PACK),
+            res[:].rearrange("p (t w) -> p t w", t=PACK)[:, :, 0:MID],
+        ]
+
+        def all_planes(lo, hi):
+            h = lo // MID
+            return halves[h][:, :, lo - h * MID : hi - h * MID]
+
+        def row(t, lo, hi):
+            start = first_at + t * MID + lo if lo < MID else t * pitch + lo - MID
+            return res[:, start : start + hi - lo]
 
         def lay_last_plane(lo, hi):
             nc.vector.tensor_copy(z_slots[:, lo:hi, PACK - 1], z[PACK - 1][:, lo:hi])
@@ -190,75 +203,72 @@ def tile_picked_sae8_relu_po_kernel(
         def decode(t, lo, hi, on_vector=False):
             acc = psum.tile([P, BANK], F32, name=f"acc2_{lo}_{t}", tag=f"bank{len(banks_used) % BANKS}")
             banks_used.append(acc)
-            nc.tensor.matmul_mx(
-                out=acc[:, 0 : hi - lo],
-                lhsT=w2_deal[:, 2 * P * t : 2 * P * (t + 1)].bitcast(FP4X4),
-                lhsT_scale=w2s_deal[:, P * t : P * (t + 1)],
-                rhs=z_codes[:, lo:hi].bitcast(FP8X4),
-                rhs_scale=z_scales[:, lo:hi],
-                start=True,
-                stop=True,
+            mx_pass(
+                acc[:, 0 : hi - lo],
+                w2_deal[:, 2 * P * t : 2 * P * (t + 1)].bitcast(FP4X4),
+                w2s_deal[:, P * t : P * (t + 1)],
+                z_codes[:, lo:hi].bitcast(FP8X4),
+                z_scales[:, lo:hi],
             )
             if on_vector:
-                nc.vector.tensor_scalar(res[:, t, lo:hi], acc[:, 0 : hi - lo], b2_sb[:, t : t + 1], None, op0=ALU.add)
+                nc.vector.tensor_scalar(row(t, lo, hi), acc[:, 0 : hi - lo], b2_sb[:, t : t + 1], None, op0=ALU.add)
             else:
-                nc.scalar.activation(res[:, t, lo:hi], acc[:, 0 : hi - lo], ACT.Identity, bias=b2_sb[:, t : t + 1])
+                nc.scalar.activation(row(t, lo, hi), acc[:, 0 : hi - lo], ACT.Identity, bias=b2_sb[:, t : t + 1])
 
         def store(t, lo, hi):
-            nc.sync.dma_start(out_rows[:, t : t + 1, lo:hi], res[:, t : t + 1, lo:hi])
+            nc.sync.dma_start(out_rows[:, t, lo:hi], row(t, lo, hi))
 
         def round_result(lo, hi, copy=nc.vector.tensor_copy):
             copy(
                 res_bf[:, lo:hi, :].rearrange("p (g i) t -> p g t i", i=4),
-                res[:, :, lo:hi].rearrange("p t (g i) -> p g t i", i=4),
+                all_planes(lo, hi).rearrange("p t (g i) -> p g t i", i=4),
             )
 
         def quantise_result(lo, hi):
             nc.vector.quantize_mx(out_words[:, lo:hi].bitcast(FP8X4), out_scales[:, lo:hi], res_bf[:, lo:hi, :].rearrange("p n t -> p (n t)"))
 
         lay_last_plane(0, EIGHTH)
-        lay_last_plane(EIGHTH, QUARTER)
+        lay_last_plane(EIGHTH, FRONT)
         quantise_z(0, EIGHTH)
         quantise_z(EIGHTH, QUARTER)
-        lay_last_plane(SPLIT, U - QUARTER)
         quantise_z(QUARTER, MID)
-        lay_last_plane(U - QUARTER, U)
-        quantise_z(MID, U - QUARTER)
-        quantise_z(U - QUARTER, U)
+        lay_last_plane(SPLIT, LAST)
+        lay_last_plane(LAST, U)
 
-        decode(0, 0, EIGHTH)
-        decode(0, EIGHTH, QUARTER)
-        store(0, 0, QUARTER)
-        decode(1, 0, QUARTER)
-        store(1, 0, QUARTER)
+        decode(3, 0, EIGHTH)
+        decode(3, EIGHTH, QUARTER)
+        store(3, 0, QUARTER)
         decode(2, 0, QUARTER)
+        quantise_z(MID, LAST)
+        quantise_z(LAST, U)
         decode(2, QUARTER, MID)
         store(2, 0, MID)
-        decode(3, 0, MID)
-        store(3, 0, MID)
-        for t in (0, 1):
-            decode(t, QUARTER, MID, on_vector=True)
-        last_pieces = [(MID, U - QUARTER), (U - QUARTER, U - EIGHTH), (U - EIGHTH, U)]
-        decode(0, MID, U - QUARTER)
-        decode(0, U - QUARTER, U)
-        store(0, QUARTER, U)
-        decode(1, MID, U)
-        store(1, QUARTER, U)
-        decode(2, MID, U)
-        store(2, MID, U)
+        decode(1, 0, MID)
+        store(1, 0, MID)
+        decode(0, 0, QUARTER, on_vector=True)
+        decode(0, QUARTER, MID)
+        store(0, 0, MID)
+        decode(3, QUARTER, MID, on_vector=True)
+        last_pieces = [(MID, LAST), (LAST, U - EIGHTH), (U - EIGHTH, U)]
+        decode(0, MID, LAST)
+        decode(0, LAST, U)
+        store(0, MID, U)
+        for t in (1, 2):
+            decode(t, MID, U)
+            store(t, MID, U)
         for lo, hi in last_pieces:
             decode(3, lo, hi)
-        store(3, MID, U)
+        store(3, QUARTER, U)
 
         for lo in (0, QUARTER):
-            nc.vector.tensor_copy(res_bf[:, lo : lo + QUARTER, :], res[:, :, lo : lo + QUARTER].rearrange("p t n -> p n t"))
+            round_result(lo, lo + QUARTER)
         round_result(*last_pieces[0])
         quantise_result(0, MID)
         nc.sync.dma_start(out_1_rows[:, 0:MID], out_words[:, 0:MID].bitcast(I32))
         round_result(*last_pieces[1])
         round_result(*last_pieces[2], copy=nc.scalar.copy)
-        quantise_result(MID, U - QUARTER)
-        quantise_result(U - QUARTER, U)
+        quantise_result(MID, LAST)
+        quantise_result(LAST, U)
         nc.scalar.dma_start(out_1_rows[:, MID:U], out_words[:, MID:U].bitcast(I32))
         for q in range(4):
             queue = nc.sync if q % 2 == 0 else nc.scalar

from contextlib import ExitStack

import concourse.mybir as mybir

K, T, S, H, U, N = 512, 2048, 512, 512, 1024, 512
FLOPS = 2 * K * H * S + 2 * H * N * U

F32 = mybir.dt.float32
BF16 = mybir.dt.bfloat16
I32 = mybir.dt.int32
U32 = mybir.dt.uint32
U16 = mybir.dt.uint16
U8 = mybir.dt.uint8
FP8X4 = mybir.dt.float8_e4m3fn_x4
FP4X4 = mybir.dt.float4_e2m1fn_x4
ACT = mybir.ActivationFunctionType
ALU = mybir.AluOpType

P = 128
PACK = 4
GROUP = 16
QUADRANT = 32
SCALE_ROWS = 16
BANK = 512
BANKS = 8
FIRST = 128
HALF = S // 2
EIGHTH = U // 8
QUARTER = U // 4
MID = U // 2
LAST = U - QUARTER
FRONT = 320
SPLIT = 640
WARM_PASSES = 4
WARM_ROWS = 32
WARM_GATE = 64


def tile_picked_sae8_relu_po_kernel(
    tc, x_words, x_scales, w1, b1, w2_words, w2_scales, b2, offs, held, out_0, out_1, out_2
):
    nc = tc.nc

    def quadrant_rows(q):
        return slice(QUADRANT * q, QUADRANT * q + 4)

    def mx_pass(out, lhsT, lhsT_scale, rhs, rhs_scale):
        nc.tensor.matmul_mx(out=out, lhsT=lhsT, lhsT_scale=lhsT_scale, rhs=rhs, rhs_scale=rhs_scale, start=True, stop=True)

    with ExitStack() as ctx:
        lists = ctx.enter_context(tc.tile_pool(name="lists", bufs=1))
        sb = ctx.enter_context(tc.tile_pool(name="sb", bufs=1))
        psum = ctx.enter_context(tc.psum_pool(name="psum", bufs=1))

        offs_sb = lists.tile([P, S // GROUP], U16, name="offs_sb")
        held_sb = lists.tile([P, S // GROUP], U16, name="held_sb")
        w1_raw = sb.tile([P, PACK, H], F32, name="w1_raw", tag="raw", align_bytes=64)
        x_tab = sb.tile([P, T], U32, name="x_tab", tag="table", align_bytes=64)
        xs_tab = sb.tile([P, T], U8, name="xs_tab", tag="rows", align_bytes=64)
        z = [sb.tile([P, U], F32, name=f"z{t}", align_bytes=64) for t in range(2)]
        xs_pick = sb.tile([P, S], U8, name="xs_pick", align_bytes=64)
        xs_rows = sb.tile([P, S], U8, name="xs_rows", align_bytes=64)

        landing = P - SCALE_ROWS
        nc.sync.dma_start(offs_sb[:], offs)
        nc.scalar.dma_start(xs_tab[landing:P, :].bitcast(I32), x_scales[0].bitcast(I32))
        nc.sync.dma_start(w1_raw[:], w1.rearrange("(p j) c -> p j c", j=PACK))
        nc.sync.dma_start(x_tab[:].bitcast(I32), x_words[0].rearrange("p c r -> p (c r)").bitcast(I32))
        nc.sync.dma_start(held_sb[:], held)

        nc.vector.memset(xs_tab[0:landing, :].bitcast(I32), 0)
        nc.vector.memset(xs_pick[:].bitcast(I32), 0)
        nc.vector.tensor_copy(xs_rows[:], xs_tab[:].indirect(offs_sb[:]))
        for q in range(4):
            nc.sync.dma_start(xs_pick[quadrant_rows(q), :].bitcast(I32), xs_rows[landing + 4 * q : landing + 4 * q + 4, :].bitcast(I32))
        b1_sb = sb.tile([P, PACK], F32, name="b1_sb", tag="rows", align_bytes=64)
        nc.sync.dma_start(b1_sb[:], b1.rearrange("(p t) o -> p (t o)", t=PACK))
        for t in range(2):
            nc.vector.memset(z[t][:], 0.0)

        w1_src = w1_raw[:].rearrange("p j (m t) -> p m j t", t=PACK)
        w1_codes = sb.tile([P, H], U32, name="w1_codes", align_bytes=64)
        w1_scales = sb.tile([P, H], U8, name="w1_scales", align_bytes=64)
        w1_bf = [sb.tile([P, 2, P, PACK], BF16, name=f"w1_bf{h}", tag=f"stage{h}", align_bytes=64) for h in range(2)]
        for h, copy in enumerate((nc.vector.tensor_copy, nc.scalar.copy)):
            copy(w1_bf[h][:].rearrange("p t m j -> p m j t"), w1_src[:, :, :, 2 * h : 2 * h + 2])
        for h in range(2):
            cols = slice(2 * P * h, 2 * P * (h + 1))
            nc.vector.quantize_mx(w1_codes[:, cols].bitcast(FP8X4), w1_scales[:, cols], w1_bf[h][:].rearrange("p t m j -> p (t m j)"))

        x_pick = sb.tile([P, S], U32, name="x_pick", align_bytes=64)
        for lo, hi in ((0, FIRST), (FIRST, S)):
            nc.vector.tensor_copy(x_pick[:, lo:hi], x_tab[:].indirect(offs_sb[:, lo // GROUP : hi // GROUP]))

        w2_raw = sb.tile([P, 2 * N], U8, name="w2_raw", tag="raw", align_bytes=64)
        w2s_raw = sb.tile([P, N], U8, name="w2s_raw", tag="stage1", align_bytes=64)
        z.append(sb.tile([P, U], F32, name="z2", tag="table", align_bytes=64))
        nc.gpsimd.memset(z[2][:], 0.0)
        w2s_deal = sb.tile([P, N], U8, name="w2s_deal", align_bytes=64)
        nc.sync.dma_start(w2_raw[:].bitcast(I32), w2_words[0].bitcast(I32))
        nc.gpsimd.memset(w2s_raw[:].bitcast(I32), 0)
        for q in range(4):
            nc.sync.dma_start(w2s_raw[quadrant_rows(q), :].bitcast(I32), w2_scales[0, 4 * q : 4 * q + 4, :].bitcast(I32))
        nc.gpsimd.tensor_copy(
            w2s_deal[:].rearrange("p (t m) -> p t m", t=PACK),
            w2s_raw[:].rearrange("p (m t) -> p t m", t=PACK),
        )

        y = [sb.tile([P, S], F32, name=f"y{t}", tag=f"y{t}", align_bytes=64) for t in range(PACK)]
        pieces = [(0, 0, FIRST), (1, 0, FIRST), (0, FIRST, S), (1, FIRST, S), (2, 0, S), (3, 0, S)]
        for i, (t, lo, hi) in enumerate(pieces):
            acc = psum.tile([P, BANK], F32, name=f"acc1_{i}", tag=f"bank{i}")
            w1_cols = slice(t * P, (t + 1) * P)
            cuts = [lo, HALF, hi] if lo == FIRST else [lo, hi]
            for n0, n1 in zip(cuts, cuts[1:]):
                mx_pass(
                    acc[:, n0 - lo : n1 - lo],
                    w1_codes[:, w1_cols].bitcast(FP8X4),
                    w1_scales[:, w1_cols],
                    x_pick[:, n0:n1].bitcast(FP8X4),
                    xs_pick[:, n0:n1],
                )
            nc.scalar.activation(y[t][:, lo:hi], acc[:, 0 : hi - lo], ACT.Relu, bias=b1_sb[:, t : t + 1])

        b2_sb = sb.tile([P, PACK], F32, name="b2_sb", tag="stage0", align_bytes=64)
        nc.sync.dma_start(b2_sb[:], b2.rearrange("(p t) o -> p (t o)", t=PACK))

        z_bf = sb.tile([P, U * PACK], BF16, name="z_bf", align_bytes=64)
        z_slots = z_bf[:].rearrange("p (w t) -> p w t", t=PACK)

        def both_slots(t, lo, hi):
            return z[t][:, lo:hi].unsqueeze(2).to_broadcast([P, hi - lo, 2])

        for t, lo, hi in pieces:
            nc.vector.tensor_copy(z[t][:].indirect(held_sb[:, lo // GROUP : hi // GROUP]), y[t][:, lo:hi])
            if hi == S and t == 0:
                z.append(sb.tile([P, U], F32, name="z3", tag="y0", align_bytes=64))
                nc.gpsimd.memset(z[3][:], 0.0)
            if hi == S and t < 2:
                nc.scalar.copy(z_slots[:, 0:SPLIT, t], z[t][:, 0:SPLIT])
                nc.gpsimd.tensor_scalar(z_slots[:, SPLIT:U, t], z[t][:, SPLIT:U], 1.0, 0.0, op0=ALU.mult, op1=ALU.add)
            if t == 2:
                w2_deal = sb.tile([P, 2 * N], U8, name="w2_deal", tag="y2", align_bytes=64)
                nc.scalar.copy(
                    w2_deal[:].bitcast(U16).rearrange("p (t m) -> p t m", t=PACK),
                    w2_raw[:].bitcast(U16).rearrange("p (m t) -> p t m", t=PACK),
                )
                unread = psum.tile([P, BANK], F32, name="unread", tag=f"bank{BANKS - 1}")
                mx_pass(
                    unread[:, 0:WARM_GATE],
                    w1_codes[:, 0:P].bitcast(FP8X4),
                    w1_scales[:, 0:P],
                    w2_deal[:, 0 : 2 * WARM_GATE].bitcast(FP4X4),
                    w2s_deal[:, 0:WARM_GATE],
                )
                for rep in range(WARM_PASSES):
                    mx_pass(
                        unread[0:WARM_ROWS, :],
                        w1_codes[:, 0:WARM_ROWS].bitcast(FP8X4),
                        w1_scales[:, 0:WARM_ROWS],
                        w1_codes[:].bitcast(FP8X4),
                        w1_scales[:],
                    )
                nc.scalar.copy(z_slots[:, 0:FRONT, t:PACK], both_slots(t, 0, FRONT))
                nc.scalar.copy(z_slots[:, FRONT:SPLIT, t], z[t][:, FRONT:SPLIT])
                nc.gpsimd.tensor_scalar(z_slots[:, SPLIT:U, t:PACK], both_slots(t, SPLIT, U), 1.0, 0.0, op0=ALU.mult, op1=ALU.add)

        for lo, hi in ((FRONT, MID), (MID, SPLIT)):
            nc.scalar.copy(z_slots[:, lo:hi, PACK - 1], z[PACK - 1][:, lo:hi])

        out_words = sb.tile([P, U], U32, name="out_words", align_bytes=64)
        out_scales = sb.tile([P, U], U8, name="out_scales", align_bytes=64)
        out_rows = out_0.rearrange("(p t) w -> p t w", t=PACK)
        out_1_rows = out_1[0].rearrange("p c r -> p (c r)").bitcast(I32)

        z_codes = sb.tile([P, U], U32, name="z_codes", align_bytes=64)
        z_scales = sb.tile([P, U], U8, name="z_scales", align_bytes=64)
        res_bf = sb.tile([P, U, PACK], BF16, name="res_bf", align_bytes=64)
        banks_used = []

        pitch = (PACK + 1) * MID
        first_at = 2 * pitch + MID
        res = sb.tile([P, PACK * pitch], F32, name="res", align_bytes=64)
        halves = [
            res[:, first_at : first_at + PACK * MID].rearrange("p (t w) -> p t w", t=PACK),
            res[:].rearrange("p (t w) -> p t w", t=PACK)[:, :, 0:MID],
        ]

        def all_planes(lo, hi):
            h = lo // MID
            return halves[h][:, :, lo - h * MID : hi - h * MID]

        def row(t, lo, hi):
            start = first_at + t * MID + lo if lo < MID else t * pitch + lo - MID
            return res[:, start : start + hi - lo]

        def lay_last_plane(lo, hi):
            nc.vector.tensor_copy(z_slots[:, lo:hi, PACK - 1], z[PACK - 1][:, lo:hi])

        def quantise_z(lo, hi):
            nc.vector.quantize_mx(z_codes[:, lo:hi].bitcast(FP8X4), z_scales[:, lo:hi], z_bf[:, PACK * lo : PACK * hi])

        def decode(t, lo, hi, on_vector=False):
            acc = psum.tile([P, BANK], F32, name=f"acc2_{lo}_{t}", tag=f"bank{len(banks_used) % BANKS}")
            banks_used.append(acc)
            mx_pass(
                acc[:, 0 : hi - lo],
                w2_deal[:, 2 * P * t : 2 * P * (t + 1)].bitcast(FP4X4),
                w2s_deal[:, P * t : P * (t + 1)],
                z_codes[:, lo:hi].bitcast(FP8X4),
                z_scales[:, lo:hi],
            )
            if on_vector:
                nc.vector.tensor_scalar(row(t, lo, hi), acc[:, 0 : hi - lo], b2_sb[:, t : t + 1], None, op0=ALU.add)
            else:
                nc.scalar.activation(row(t, lo, hi), acc[:, 0 : hi - lo], ACT.Identity, bias=b2_sb[:, t : t + 1])

        def store(t, lo, hi):
            nc.sync.dma_start(out_rows[:, t, lo:hi], row(t, lo, hi))

        def round_result(lo, hi, copy=nc.vector.tensor_copy):
            copy(
                res_bf[:, lo:hi, :].rearrange("p (g i) t -> p g t i", i=4),
                all_planes(lo, hi).rearrange("p t (g i) -> p g t i", i=4),
            )

        def quantise_result(lo, hi):
            nc.vector.quantize_mx(out_words[:, lo:hi].bitcast(FP8X4), out_scales[:, lo:hi], res_bf[:, lo:hi, :].rearrange("p n t -> p (n t)"))

        lay_last_plane(0, EIGHTH)
        lay_last_plane(EIGHTH, FRONT)
        quantise_z(0, EIGHTH)
        quantise_z(EIGHTH, QUARTER)
        quantise_z(QUARTER, MID)
        lay_last_plane(SPLIT, LAST)
        lay_last_plane(LAST, U)

        decode(3, 0, EIGHTH)
        decode(3, EIGHTH, QUARTER)
        store(3, 0, QUARTER)
        decode(2, 0, QUARTER)
        quantise_z(MID, LAST)
        quantise_z(LAST, U)
        decode(2, QUARTER, MID)
        store(2, 0, MID)
        decode(1, 0, MID)
        store(1, 0, MID)
        decode(0, 0, QUARTER, on_vector=True)
        decode(0, QUARTER, MID)
        store(0, 0, MID)
        decode(3, QUARTER, MID, on_vector=True)
        last_pieces = [(MID, LAST), (LAST, U - EIGHTH), (U - EIGHTH, U)]
        decode(0, MID, LAST)
        decode(0, LAST, U)
        store(0, MID, U)
        for t in (1, 2):
            decode(t, MID, U)
            store(t, MID, U)
        for lo, hi in last_pieces:
            decode(3, lo, hi)
        store(3, QUARTER, U)

        for lo in (0, QUARTER):
            round_result(lo, lo + QUARTER)
        round_result(*last_pieces[0])
        quantise_result(0, MID)
        nc.sync.dma_start(out_1_rows[:, 0:MID], out_words[:, 0:MID].bitcast(I32))
        round_result(*last_pieces[1])
        round_result(*last_pieces[2], copy=nc.scalar.copy)
        quantise_result(MID, LAST)
        quantise_result(LAST, U)
        nc.scalar.dma_start(out_1_rows[:, MID:U], out_words[:, MID:U].bitcast(I32))
        for q in range(4):
            queue = nc.sync if q % 2 == 0 else nc.scalar
            queue.dma_start(out_2[0, 4 * q : 4 * q + 4, :].bitcast(I32), out_scales[quadrant_rows(q), :].bitcast(I32))
